import numpy as np
import ml_dtypes


def mxq(x, axis, fmt="e4m3"):
    dtype, down = {"e4m3": (ml_dtypes.float8_e4m3fn, 7), "e5m2": (ml_dtypes.float8_e5m2, 14)}[fmt]
    v = np.moveaxis(np.asarray(x, np.float32).astype(ml_dtypes.bfloat16).astype(np.float64), axis, -1)
    blocks = v.reshape(v.shape[:-1] + (-1, 32))
    amax = np.abs(blocks).max(-1, keepdims=True)
    byte = np.maximum(np.where(amax > 0, np.frexp(amax)[1] - 1 + 127, 0) - down, 1)
    scale = np.exp2(byte - 127.0)
    codes = (blocks / scale).astype(np.float32).astype(dtype).astype(np.float64)
    return np.moveaxis((codes * scale).reshape(v.shape), -1, axis)


WIDE = False


def mx_kscale(k):
    if not WIDE:
        return np.ones(k)
    levels = np.array([10, -10, 5, -5, 0])
    if k % 512:
        return np.exp2(np.random.permutation(np.resize(levels, k // 32))).repeat(32)
    a = np.empty((k // 512, 16))
    for p in range(k // 512):
        a[p, :8] = np.random.permutation(np.resize(levels, 8))
        for g in range(8):
            far = levels[np.abs(levels - a[p, g]) >= 10]
            a[p, g + 8] = far[np.random.randint(len(far))]
    return np.exp2(a.ravel()).repeat(32)


def f64(x):
    return np.asarray(x).astype(np.float64)


def striped(idx):
    return np.tile(idx.reshape(-1, 16).T, (8, 1)).astype(np.uint16)


def unstriped(offs):
    return offs[:16].T.reshape(-1).astype(np.int64)


E2M1 = np.array([0.0, 0.5, 1.0, 1.5, 2.0, 3.0, 4.0, 6.0, -0.0, -0.5, -1.0, -1.5, -2.0, -3.0, -4.0, -6.0])


def pack_weight(w, fmt):
    k, n = w.shape
    w = f64(np.asarray(w, np.float32).astype(ml_dtypes.bfloat16)).reshape(k // 32, 32, n)
    amax = np.abs(w).max(1)
    if fmt == "e4m3":
        byte = np.frexp(amax)[1] - 1 + 127 - 7
    else:
        mant, ex = np.frexp(amax / 6.0)
        byte = np.where(mant > 0.5, ex, ex - 1) + 127
    byte = np.clip(np.where(amax > 0, byte, 1), 1, 254)
    scaled = (w * np.exp2(127.0 - byte)[:, None, :]).reshape(k, n).astype(np.float32)
    by_word = np.ascontiguousarray(scaled.reshape(k // 512, 128, 4, n).transpose(0, 1, 3, 2))
    if fmt == "e4m3":
        words = by_word.astype(ml_dtypes.float8_e4m3fn).view(np.uint8)
    else:
        c = by_word.astype(ml_dtypes.float4_e2m1fn).view(np.uint8) & 0xF
        words = (c[..., 0::2] | (c[..., 1::2] << 4)).reshape(k // 512, 128, 2 * n)
    return np.ascontiguousarray(words), np.ascontiguousarray(byte.astype(np.uint8).reshape(k // 512, 16, n))


def unpack_weight(words, scales, fmt):
    g, _, n = scales.shape
    words = np.ascontiguousarray(words).reshape(g, 128, n, -1)
    if fmt == "e4m3":
        vals = words.view(ml_dtypes.float8_e4m3fn).astype(np.float64)
    else:
        nib = np.empty((g, 128, n, 4), np.uint8)
        nib[..., 0::2] = words & 0xF
        nib[..., 1::2] = words >> 4
        vals = E2M1[nib]
    vals = vals * np.repeat(np.exp2(scales.astype(np.float64) - 127.0), 8, axis=1)[..., None]
    return vals.transpose(0, 1, 3, 2).reshape(g * 512, n)


def planes(y):
    n, m = y.shape
    v = y.astype(np.float32).astype(ml_dtypes.bfloat16).astype(np.float64).reshape(n // 32, 32, m)
    top = np.abs(v).max(1)
    byte = np.clip(np.where(top > 0, np.frexp(top)[1] - 1 + 127 - 7, 1), 1, 254)
    codes = (v * np.exp2(127.0 - byte)[:, None, :]).reshape(n, m).astype(np.float32).astype(ml_dtypes.float8_e4m3fn).view(np.uint8)
    words = codes.reshape(n // 512, 128, 4, m).transpose(0, 1, 3, 2)
    return np.ascontiguousarray(words), np.ascontiguousarray(byte.astype(np.uint8).reshape(n // 512, 16, m))


def relu(v):
    return np.maximum(v, 0.0)


K, T, E, C, H, N = 1024, 768, 3, 256, 512, 512


def by_expert(wq, xq):
    return np.concatenate([wq[e].T @ xq[:, e * C:(e + 1) * C] for e in range(E)], axis=1)


def setup_inputs():
    n = np.random.standard_normal
    s = mx_kscale(K)
    u = mx_kscale(H)
    slot_token = np.concatenate([np.random.permutation(T)[:C] for e in range(E)])
    x = pack_weight(n((K, T)) * s[:, None], "e4m3")
    w = [pack_weight(m, "e2m1") for m in n((E, K, N)) / np.sqrt(K) / s[None, :, None]]
    wa = [pack_weight(m, "e4m3") for m in n((E, K, H)) / np.sqrt(K) / s[None, :, None] * u]
    wb = [pack_weight(m, "e4m3") for m in n((E, H, N)) / np.sqrt(H) / u[None, :, None]]
    return {
        "x_words": x[0],
        "x_scales": x[1],
        "w_words": np.stack([m[0] for m in w]),
        "w_scales": np.stack([m[1] for m in w]),
        "wa_words": np.stack([m[0] for m in wa]),
        "wa_scales": np.stack([m[1] for m in wa]),
        "wb_words": np.stack([m[0] for m in wb]),
        "wb_scales": np.stack([m[1] for m in wb]),
        "offs": striped(slot_token),
    }


def reference(x_words, x_scales, w_words, w_scales, wa_words, wa_scales, wb_words, wb_scales, offs):
    w = np.stack([unpack_weight(w_words[e], w_scales[e], "e2m1") for e in range(E)])
    wa = np.stack([unpack_weight(wa_words[e], wa_scales[e], "e4m3") for e in range(E)])
    wb = np.stack([unpack_weight(wb_words[e], wb_scales[e], "e4m3") for e in range(E)])
    idx = unstriped(offs)
    xq = unpack_weight(x_words, x_scales, "e4m3")[:, idx]
    h = relu(by_expert(wa, xq))
    y = by_expert(w, xq) + by_expert(wb, mxq(h, 0, "e4m3"))
    out = y
    out_0 = out
    return (out_0,) + planes(out_0)

@@ -1,0 +1,238 @@
+from contextlib import ExitStack
+
+import concourse.mybir as mybir
+from concourse.masks import make_identity
+
+K, T, E, C, H, N = 1024, 768, 3, 256, 512, 512
+S = E * C
+FLOPS = 2 * S * (K * H + K * N + H * N)
+
+F32 = mybir.dt.float32
+BF16 = mybir.dt.bfloat16
+I32 = mybir.dt.int32
+U32 = mybir.dt.uint32
+U16 = mybir.dt.uint16
+U8 = mybir.dt.uint8
+FP8X4 = mybir.dt.float8_e4m3fn_x4
+FP4X4 = mybir.dt.float4_e2m1fn_x4
+RELU = mybir.ActivationFunctionType.Relu
+
+P = 128
+PACK = 4
+PASSES = K // (P * PACK)
+TILES = S // P
+PER = C // P
+WINDOW = 1024
+WA_ROW = 12
+WB_ROW = 4
+SHIFT_ROWS = 100
+
+
+def tile_moe_elr_s_relu_kernel(
+    tc, x_words, x_scales, w_words, w_scales, wa_words, wa_scales, wb_words, wb_scales, offs, out_0, out_1, out_2
+):
+    nc = tc.nc
+    with ExitStack() as ctx:
+        keep = ctx.enter_context(tc.tile_pool(name="keep", bufs=1))
+        psum = ctx.enter_context(tc.psum_pool(name="psum", bufs=1))
+
+        def held(shape, dtype, name):
+            return keep.tile(shape, dtype, name=name, align_bytes=64)
+
+        offsets = keep.tile([P, S // 16], U16, name="offsets")
+        xs_window = keep.tile([P, WINDOW], U8, name="xs_window", tag="reused", align_bytes=64)
+        wa_sc = held([P, E * PASSES, H], U8, "wa_sc")
+        y_sc_raw = held([P, E, PASSES, N], U8, "y_sc_raw")
+        xs_shift = held([P, S], U8, "xs_shift")
+        xs = held([P, S], U8, "xs")
+        ident = held([P, P], F32, "ident")
+        x_raw = [held([P, T], I32, f"x_raw{s}") for s in range(PASSES)]
+        early = [held([P, PASSES * H], I32, f"early{i}") for i in range(3)]
+        xg = [[held([P, C], U32, f"xg{e}_{s}") for s in range(PASSES)] for e in range(E)]
+        w = [held([P, PASSES, 2 * N], U8, f"w{e}") for e in range(E)]
+        wb = [held([P, N], I32, f"wb{e}") for e in range(E)]
+        y_sc = [held([P, PASSES, N], U8, f"y_sc{e}") for e in range(E)]
+        hq = [held([P, C], U32, f"hq{e}") for e in range(E)]
+        hq_sc = [held([P, C], U8, f"hq_sc{e}") for e in range(E)]
+        yq = held([P, S], U32, "yq")
+        yq_sc = held([P, S], U8, "yq_sc")
+
+        nc.gpsimd.memset(xs_window[:].bitcast(I32), 0)
+        nc.vector.memset(wa_sc[:].bitcast(I32), 0)
+        nc.vector.memset(y_sc_raw[:].bitcast(I32), 0)
+        nc.vector.memset(xs_shift[:].bitcast(I32), 0)
+
+        def load_wa(e):
+            nc.sync.dma_start(
+                wa[e].rearrange("p (s i) -> p s i", s=PASSES), wa_words[e].rearrange("s p i d -> p s (i d)").bitcast(I32)
+            )
+
+        def load_y_words(e):
+            nc.sync.dma_start(
+                w_raw[e].rearrange("p (s b) -> p s b", s=PASSES), w_words[e].rearrange("s p b -> p s b").bitcast(I32)
+            )
+            nc.sync.dma_start(wb_raw[e], wb_words[e, 0].rearrange("p n d -> p (n d)").bitcast(I32))
+
+        wa = [early[0][:], early[1][:]]
+        w_raw = [early[2][:, 0:N]]
+        wb_raw = [early[2][:, N : 2 * N]]
+        nc.sync.dma_start(offsets[:], offs)
+        for q in range(4):
+            nc.sync.dma_start(
+                xs_window[32 * q : 32 * q + 4 * PASSES, 0:T].bitcast(I32), x_scales[:, 4 * q : 4 * q + 4, :].bitcast(I32)
+            )
+        for s in range(PASSES):
+            nc.sync.dma_start(x_raw[s][:], x_words[s].rearrange("p t d -> p (t d)").bitcast(I32))
+        load_wa(0)
+        load_wa(1)
+        load_y_words(0)
+        for q in range(4):
+            nc.gpsimd.dma_start(
+                wa_sc[32 * q + WA_ROW : 32 * q + WA_ROW + 4, :, :].bitcast(I32),
+                wa_scales.rearrange("e s b i -> b (e s) i")[4 * q : 4 * q + 4].bitcast(I32),
+            )
+        for r in range(4):
+            nc.sync.dma_start(
+                y_sc_raw[32 * r + WB_ROW : 32 * r + WB_ROW + 4, :, 0, :].bitcast(I32),
+                wb_scales[:, 0].rearrange("e b n -> b e n")[4 * r : 4 * r + 4].bitcast(I32),
+            )
+        for r in range(4):
+            nc.sync.dma_start(
+                y_sc_raw[32 * r : 32 * r + 4].rearrange("q e s n -> q (e s) n").bitcast(I32),
+                w_scales.rearrange("e s b n -> b (e s) n")[4 * r : 4 * r + 4].bitcast(I32),
+            )
+
+        make_identity(nc, ident[:])
+
+        nc.vector.tensor_copy(xs[:], xs_window[:].indirect(offsets[:]))
+        nc.scalar.dma_start(xs_shift[0:SHIFT_ROWS, :].bitcast(I32), xs[4 : 4 + SHIFT_ROWS, :].bitcast(I32))
+
+        late = keep.tile([P, PASSES * H + 2 * (E - 1) * N], I32, name="late", tag="reused", align_bytes=64)
+        wa.append(late[:, 0 : PASSES * H])
+        y_words = late[:, PASSES * H :]
+        w_raw.extend(y_words[:, 2 * i * N : (2 * i + 1) * N] for i in range(E - 1))
+        wb_raw.extend(y_words[:, (2 * i + 1) * N : (2 * i + 2) * N] for i in range(E - 1))
+        load_wa(2)
+        for e in range(1, E):
+            load_y_words(e)
+        for e in range(E):
+            for s in range(PASSES):
+                nc.vector.tensor_copy(
+                    xg[e][s][:], x_raw[s][:].bitcast(U32).indirect(offsets[:, e * C // 16 : (e + 1) * C // 16])
+                )
+
+        h_pairs = {}
+
+        def h_product(u):
+            e, a = divmod(u, PER)
+            bank = psum.tile([P, H], F32, name="h_bank", bufs=3)
+            for s in range(PASSES):
+                nc.tensor.matmul_mx(
+                    out=bank[:],
+                    lhsT=xg[e][s][:, a * P : (a + 1) * P].bitcast(FP8X4),
+                    lhsT_scale=xs[4 * s : P, u * P : (u + 1) * P],
+                    rhs=wa[e][:, s * H : (s + 1) * H].bitcast(FP8X4),
+                    rhs_scale=wa_sc[WA_ROW:P, e * PASSES + s, :],
+                    start=(s == 0),
+                    stop=(s == PASSES - 1),
+                )
+            h_pairs[u] = held([P, H], BF16, f"h_pairs{u}")
+            nc.scalar.activation(
+                h_pairs[u][:].rearrange("j (v p d) -> j v p d", v=2, d=2),
+                bank[:].rearrange("j (p v d) -> j v p d", v=2, d=2),
+                RELU,
+            )
+
+        def h_turn(e):
+            bank = psum.tile([P, PER, 2, P], F32, name="ht_bank", bufs=2)
+            for a in range(PER):
+                words = h_pairs[e * PER + a][:].bitcast(F32)
+                for v in range(2):
+                    nc.tensor.transpose(bank[:, a, v, :], words[:, v * P : (v + 1) * P], ident[:])
+            grouped = held([P, C * PACK], BF16, f"h_grouped{e}")
+            nc.scalar.copy(
+                grouped[:].bitcast(F32).rearrange("p (a j v) -> p a j v", a=PER, v=2),
+                bank[:].rearrange("p a v j -> p a j v"),
+            )
+            return grouped
+
+        def h_quantize(e, grouped):
+            nc.vector.quantize_mx(out=hq[e][:].bitcast(FP8X4), scales=hq_sc[e][:], in_=grouped[:])
+
+        def deal(e):
+            nc.vector.tensor_copy(
+                w[e][:].bitcast(U16).rearrange("p s (t m) -> p s m t", t=PACK),
+                w_raw[e].bitcast(U16).rearrange("p (s m t) -> p s m t", s=PASSES, t=PACK),
+            )
+            nc.vector.tensor_copy(
+                wb[e][:].rearrange("p (t m) -> p m t", t=PACK), wb_raw[e].rearrange("p (m t) -> p m t", t=PACK)
+            )
+            nc.vector.tensor_copy(
+                y_sc[e][:].rearrange("p s (t m) -> p s m t", t=PACK),
+                y_sc_raw[:, e].rearrange("p s (m t) -> p s m t", t=PACK),
+            )
+
+        def y_product(u):
+            e, a = divmod(u, PER)
+            own = slice(a * P, (a + 1) * P)
+            cols = slice(u * P, (u + 1) * P)
+            bank = psum.tile([P, PACK, P], F32, name="y_bank", bufs=3)
+            for t in range(PACK):
+                n_cols = slice(t * P, (t + 1) * P)
+                for s in range(PASSES):
+                    nc.tensor.matmul_mx(
+                        out=bank[:, t, :],
+                        lhsT=w[e][:, s, 2 * t * P : 2 * (t + 1) * P].bitcast(FP4X4),
+                        lhsT_scale=y_sc[e][:, s, n_cols],
+                        rhs=xg[e][s][:, own].bitcast(FP8X4),
+                        rhs_scale=(xs, xs_shift)[s][:, cols],
+                        start=(s == 0),
+                        stop=False,
+                    )
+                nc.tensor.matmul_mx(
+                    out=bank[:, t, :],
+                    lhsT=wb[e][:, n_cols].bitcast(FP8X4),
+                    lhsT_scale=y_sc[e][WB_ROW:P, 0, n_cols],
+                    rhs=hq[e][:, own].bitcast(FP8X4),
+                    rhs_scale=hq_sc[e][:, own],
+                    start=False,
+                    stop=True,
+                )
+            y = held([P, PACK, P], F32, f"y{u}")
+            nc.scalar.copy(y[:], bank[:])
+            nc.sync.dma_start(out_0.rearrange("(p t) j -> p t j", t=PACK)[:, :, cols], y[:])
+            return y
+
+        def y_round(u, y):
+            grouped = held([P, P * PACK], BF16, f"y_grouped{u}")
+            nc.vector.tensor_copy(
+                grouped[:].rearrange("p (c i t) -> p c t i", i=4, t=PACK),
+                y[:].rearrange("p t (c i) -> p c t i", i=4),
+            )
+            return grouped
+
+        def y_quantize(u, grouped):
+            cols = slice(u * P, (u + 1) * P)
+            nc.vector.quantize_mx(out=yq[:, cols].bitcast(FP8X4), scales=yq_sc[:, cols], in_=grouped[:])
+            nc.sync.dma_start(out_1[0].rearrange("p j d -> p (j d)").bitcast(I32)[:, cols], yq[:, cols].bitcast(I32))
+
+        h_grouped = {}
+        for u in range(4):
+            h_product(u)
+        h_grouped[0] = h_turn(0)
+        for u in range(4, 6):
+            h_product(u)
+        h_grouped[1] = h_turn(1)
+        h_grouped[2] = h_turn(2)
+        deal(0)
+        h_quantize(0, h_grouped[0])
+        for e in range(E):
+            ys = [y_product(e * PER + a) for a in range(PER)]
+            if e + 1 < E:
+                deal(e + 1)
+                h_quantize(e + 1, h_grouped[e + 1])
+            gs = [y_round(e * PER + a, ys[a]) for a in range(PER)]
+            for a in range(PER):
+                y_quantize(e * PER + a, gs[a])
+        for r in range(4):
+            (nc.sync, nc.scalar)[r % 2].dma_start(out_2[0, 4 * r : 4 * r + 4, :].bitcast(I32), yq_sc[32 * r : 32 * r + 4, :].bitcast(I32))

@@ -161,15 +161,16 @@ def tile_moe_elr_s_relu_kernel(
 
         def deal(e):
             nc.vector.tensor_copy(
-                w[e][:].bitcast(U16).rearrange("p s (t m) -> p s m t", t=PACK),
-                w_raw[e].bitcast(U16).rearrange("p (s m t) -> p s m t", s=PASSES, t=PACK),
+                w[e][:].bitcast(U16).rearrange("p s (t m) -> p s t m", t=PACK),
+                w_raw[e].bitcast(U16).rearrange("p (s m t) -> p s t m", s=PASSES, t=PACK),
             )
             nc.vector.tensor_copy(
-                wb[e][:].rearrange("p (t m) -> p m t", t=PACK), wb_raw[e].rearrange("p (m t) -> p m t", t=PACK)
+                wb[e][:].rearrange("p (t c i) -> p c t i", t=PACK, i=4),
+                wb_raw[e].rearrange("p (c i t) -> p c t i", t=PACK, i=4),
             )
             nc.vector.tensor_copy(
-                y_sc[e][:].rearrange("p s (t m) -> p s m t", t=PACK),
-                y_sc_raw[:, e].rearrange("p s (m t) -> p s m t", t=PACK),
+                y_sc[e][:].rearrange("p s (t m) -> p s t m", t=PACK),
+                y_sc_raw[:, e].rearrange("p s (m t) -> p s t m", t=PACK),
             )
 
         def y_product(u):

@@ -42,24 +42,24 @@ def tile_moe_elr_s_relu_kernel(
         offsets = keep.tile([P, S // 16], U16, name="offsets")
         xs_window = keep.tile([P, WINDOW], U8, name="xs_window", tag="reused", align_bytes=64)
         wa_sc = held([P, E * PASSES, H], U8, "wa_sc")
-        y_sc_raw = held([P, E, PASSES, N], U8, "y_sc_raw")
+        y_sc_raw = keep.tile([P, E * PASSES * N], U8, name="y_sc_raw", tag="raw_scales", align_bytes=64)
         xs_shift = held([P, S], U8, "xs_shift")
         xs = held([P, S], U8, "xs")
         ident = held([P, P], F32, "ident")
         x_raw = [held([P, T], I32, f"x_raw{s}") for s in range(PASSES)]
-        early = [held([P, PASSES * H], I32, f"early{i}") for i in range(3)]
+        early = [held([P, PASSES * H], I32, f"early{i}") for i in range(4)]
         xg = [[held([P, C], U32, f"xg{e}_{s}") for s in range(PASSES)] for e in range(E)]
         w = [held([P, PASSES, 2 * N], U8, f"w{e}") for e in range(E)]
         wb = [held([P, N], I32, f"wb{e}") for e in range(E)]
-        y_sc = [held([P, PASSES, N], U8, f"y_sc{e}") for e in range(E)]
-        hq = [held([P, C], U32, f"hq{e}") for e in range(E)]
+        y_sc = held([P, E * PASSES, N], U8, "y_sc")
         hq_sc = [held([P, C], U8, f"hq_sc{e}") for e in range(E)]
         yq = held([P, S], U32, "yq")
         yq_sc = held([P, S], U8, "yq_sc")
 
-        nc.gpsimd.memset(xs_window[:].bitcast(I32), 0)
+        nc.vector.memset(xs_window[:].bitcast(I32), 0)
         nc.vector.memset(wa_sc[:].bitcast(I32), 0)
         nc.vector.memset(y_sc_raw[:].bitcast(I32), 0)
+        make_identity(nc, ident[:])
         nc.vector.memset(xs_shift[:].bitcast(I32), 0)
 
         def load_wa(e):
@@ -73,9 +73,9 @@ def tile_moe_elr_s_relu_kernel(
             )
             nc.sync.dma_start(wb_raw[e], wb_words[e, 0].rearrange("p n d -> p (n d)").bitcast(I32))
 
-        wa = [early[0][:], early[1][:]]
-        w_raw = [early[2][:, 0:N]]
-        wb_raw = [early[2][:, N : 2 * N]]
+        wa = [early[e][:] for e in range(E)]
+        w_raw = [early[3][:, 0:N]]
+        wb_raw = [early[3][:, N : 2 * N]]
         nc.sync.dma_start(offsets[:], offs)
         for q in range(4):
             nc.sync.dma_start(
@@ -84,35 +84,32 @@ def tile_moe_elr_s_relu_kernel(
         for s in range(PASSES):
             nc.sync.dma_start(x_raw[s][:], x_words[s].rearrange("p t d -> p (t d)").bitcast(I32))
         load_wa(0)
-        load_wa(1)
-        load_y_words(0)
         for q in range(4):
-            nc.gpsimd.dma_start(
+            nc.sync.dma_start(
                 wa_sc[32 * q + WA_ROW : 32 * q + WA_ROW + 4, :, :].bitcast(I32),
                 wa_scales.rearrange("e s b i -> b (e s) i")[4 * q : 4 * q + 4].bitcast(I32),
             )
+        load_wa(1)
+        load_wa(2)
+        load_y_words(0)
         for r in range(4):
             nc.sync.dma_start(
-                y_sc_raw[32 * r + WB_ROW : 32 * r + WB_ROW + 4, :, 0, :].bitcast(I32),
+                y_sc_raw[32 * r + WB_ROW : 32 * r + WB_ROW + 4, 0 : E * N].bitcast(I32).rearrange("q (e n) -> q e n", e=E),
                 wb_scales[:, 0].rearrange("e b n -> b e n")[4 * r : 4 * r + 4].bitcast(I32),
             )
         for r in range(4):
             nc.sync.dma_start(
-                y_sc_raw[32 * r : 32 * r + 4].rearrange("q e s n -> q (e s) n").bitcast(I32),
+                y_sc_raw[32 * r : 32 * r + 4, :].bitcast(I32).rearrange("q (g n) -> q g n", g=E * PASSES),
                 w_scales.rearrange("e s b n -> b (e s) n")[4 * r : 4 * r + 4].bitcast(I32),
             )
 
-        make_identity(nc, ident[:])
-
         nc.vector.tensor_copy(xs[:], xs_window[:].indirect(offsets[:]))
-        nc.scalar.dma_start(xs_shift[0:SHIFT_ROWS, :].bitcast(I32), xs[4 : 4 + SHIFT_ROWS, :].bitcast(I32))
+        nc.sync.dma_start(xs_shift[0:SHIFT_ROWS, :].bitcast(I32), xs[4 : 4 + SHIFT_ROWS, :].bitcast(I32))
 
-        late = keep.tile([P, PASSES * H + 2 * (E - 1) * N], I32, name="late", tag="reused", align_bytes=64)
-        wa.append(late[:, 0 : PASSES * H])
-        y_words = late[:, PASSES * H :]
+        late = keep.tile([P, 2 * (E - 1) * N], I32, name="late", tag="reused", align_bytes=64)
+        y_words = late[:]
         w_raw.extend(y_words[:, 2 * i * N : (2 * i + 1) * N] for i in range(E - 1))
         wb_raw.extend(y_words[:, (2 * i + 1) * N : (2 * i + 2) * N] for i in range(E - 1))
-        load_wa(2)
         for e in range(1, E):
             load_y_words(e)
         for e in range(E):
@@ -125,7 +122,7 @@ def tile_moe_elr_s_relu_kernel(
 
         def h_product(u):
             e, a = divmod(u, PER)
-            bank = psum.tile([P, H], F32, name="h_bank", bufs=3)
+            bank = psum.tile([P, H], F32, name="h_bank", tag="sums", bufs=4)
             for s in range(PASSES):
                 nc.tensor.matmul_mx(
                     out=bank[:],
@@ -157,7 +154,7 @@ def tile_moe_elr_s_relu_kernel(
             return grouped
 
         def h_quantize(e, grouped):
-            nc.vector.quantize_mx(out=hq[e][:].bitcast(FP8X4), scales=hq_sc[e][:], in_=grouped[:])
+            nc.vector.quantize_mx(out=hq[e].bitcast(FP8X4), scales=hq_sc[e][:], in_=grouped[:])
 
         def deal(e):
             nc.vector.tensor_copy(
@@ -168,23 +165,19 @@ def tile_moe_elr_s_relu_kernel(
                 wb[e][:].rearrange("p (t c i) -> p c t i", t=PACK, i=4),
                 wb_raw[e].rearrange("p (c i t) -> p c t i", t=PACK, i=4),
             )
-            nc.vector.tensor_copy(
-                y_sc[e][:].rearrange("p s (t m) -> p s t m", t=PACK),
-                y_sc_raw[:, e].rearrange("p s (m t) -> p s t m", t=PACK),
-            )
 
         def y_product(u):
             e, a = divmod(u, PER)
             own = slice(a * P, (a + 1) * P)
             cols = slice(u * P, (u + 1) * P)
-            bank = psum.tile([P, PACK, P], F32, name="y_bank", bufs=3)
+            bank = psum.tile([P, PACK, P], F32, name="y_bank", tag="sums", bufs=4)
             for t in range(PACK):
                 n_cols = slice(t * P, (t + 1) * P)
                 for s in range(PASSES):
                     nc.tensor.matmul_mx(
                         out=bank[:, t, :],
                         lhsT=w[e][:, s, 2 * t * P : 2 * (t + 1) * P].bitcast(FP4X4),
-                        lhsT_scale=y_sc[e][:, s, n_cols],
+                        lhsT_scale=y_sc[:, e * PASSES + s, n_cols],
                         rhs=xg[e][s][:, own].bitcast(FP8X4),
                         rhs_scale=(xs, xs_shift)[s][:, cols],
                         start=(s == 0),
@@ -193,22 +186,18 @@ def tile_moe_elr_s_relu_kernel(
                 nc.tensor.matmul_mx(
                     out=bank[:, t, :],
                     lhsT=wb[e][:, n_cols].bitcast(FP8X4),
-                    lhsT_scale=y_sc[e][WB_ROW:P, 0, n_cols],
+                    lhsT_scale=y_sc[WB_ROW:P, e, n_cols],
                     rhs=hq[e][:, own].bitcast(FP8X4),
                     rhs_scale=hq_sc[e][:, own],
                     start=False,
                     stop=True,
                 )
             y = held([P, PACK, P], F32, f"y{u}")
+            grouped = held([P, P * PACK], BF16, f"y_grouped{u}")
             nc.scalar.copy(y[:], bank[:])
             nc.sync.dma_start(out_0.rearrange("(p t) j -> p t j", t=PACK)[:, :, cols], y[:])
-            return y
-
-        def y_round(u, y):
-            grouped = held([P, P * PACK], BF16, f"y_grouped{u}")
             nc.vector.tensor_copy(
-                grouped[:].rearrange("p (c i t) -> p c t i", i=4, t=PACK),
-                y[:].rearrange("p t (c i) -> p c t i", i=4),
+                grouped[:].rearrange("p (c i t) -> p c t i", i=4, t=PACK), y[:].rearrange("p t (c i) -> p c t i", i=4)
             )
             return grouped
 
@@ -226,14 +215,19 @@ def tile_moe_elr_s_relu_kernel(
         h_grouped[1] = h_turn(1)
         h_grouped[2] = h_turn(2)
         deal(0)
+        nc.vector.tensor_copy(
+            y_sc[:].rearrange("p g (t m) -> p g t m", t=PACK),
+            y_sc_raw[:].rearrange("p (g m t) -> p g t m", g=E * PASSES, t=PACK),
+        )
+        hq_all = keep.tile([P, S], U32, name="hq_all", tag="raw_scales", align_bytes=64)
+        hq = [hq_all[:, e * C : (e + 1) * C] for e in range(E)]
         h_quantize(0, h_grouped[0])
         for e in range(E):
             ys = [y_product(e * PER + a) for a in range(PER)]
             if e + 1 < E:
                 deal(e + 1)
                 h_quantize(e + 1, h_grouped[e + 1])
-            gs = [y_round(e * PER + a, ys[a]) for a in range(PER)]
             for a in range(PER):
-                y_quantize(e * PER + a, gs[a])
+                y_quantize(e * PER + a, ys[a])
         for r in range(4):
             (nc.sync, nc.scalar)[r % 2].dma_start(out_2[0, 4 * r : 4 * r + 4, :].bitcast(I32), yq_sc[32 * r : 32 * r + 4, :].bitcast(I32))

@@ -41,13 +41,14 @@ def tile_moe_elr_s_relu_kernel(
 
         offsets = keep.tile([P, S // 16], U16, name="offsets")
         xs_window = keep.tile([P, WINDOW], U8, name="xs_window", tag="reused", align_bytes=64)
+        xs_rows = held([P, T], U8, "xs_rows")
         wa_sc = held([P, E * PASSES, H], U8, "wa_sc")
         y_sc_raw = keep.tile([P, E * PASSES * N], U8, name="y_sc_raw", tag="raw_scales", align_bytes=64)
         xs_shift = held([P, S], U8, "xs_shift")
         xs = held([P, S], U8, "xs")
         ident = held([P, P], F32, "ident")
         x_raw = [held([P, T], I32, f"x_raw{s}") for s in range(PASSES)]
-        early = [held([P, PASSES * H], I32, f"early{i}") for i in range(4)]
+        early = [held([P, PASSES * H], I32, f"early{i}") for i in range(E)]
         xg = [[held([P, C], U32, f"xg{e}_{s}") for s in range(PASSES)] for e in range(E)]
         w = [held([P, PASSES, 2 * N], U8, f"w{e}") for e in range(E)]
         wb = [held([P, N], I32, f"wb{e}") for e in range(E)]
@@ -56,7 +57,7 @@ def tile_moe_elr_s_relu_kernel(
         yq = held([P, S], U32, "yq")
         yq_sc = held([P, S], U8, "yq_sc")
 
-        nc.vector.memset(xs_window[:].bitcast(I32), 0)
+        nc.gpsimd.memset(xs_window[:].bitcast(I32), 0)
         nc.vector.memset(wa_sc[:].bitcast(I32), 0)
         nc.vector.memset(y_sc_raw[:].bitcast(I32), 0)
         make_identity(nc, ident[:])
@@ -74,24 +75,21 @@ def tile_moe_elr_s_relu_kernel(
             nc.sync.dma_start(wb_raw[e], wb_words[e, 0].rearrange("p n d -> p (n d)").bitcast(I32))
 
         wa = [early[e][:] for e in range(E)]
-        w_raw = [early[3][:, 0:N]]
-        wb_raw = [early[3][:, N : 2 * N]]
         nc.sync.dma_start(offsets[:], offs)
         for q in range(4):
             nc.sync.dma_start(
-                xs_window[32 * q : 32 * q + 4 * PASSES, 0:T].bitcast(I32), x_scales[:, 4 * q : 4 * q + 4, :].bitcast(I32)
+                xs_rows[32 * q : 32 * q + 4 * PASSES, :].bitcast(I32), x_scales[:, 4 * q : 4 * q + 4, :].bitcast(I32)
             )
         for s in range(PASSES):
             nc.sync.dma_start(x_raw[s][:], x_words[s].rearrange("p t d -> p (t d)").bitcast(I32))
         load_wa(0)
         for q in range(4):
-            nc.sync.dma_start(
+            nc.scalar.dma_start(
                 wa_sc[32 * q + WA_ROW : 32 * q + WA_ROW + 4, :, :].bitcast(I32),
                 wa_scales.rearrange("e s b i -> b (e s) i")[4 * q : 4 * q + 4].bitcast(I32),
             )
         load_wa(1)
         load_wa(2)
-        load_y_words(0)
         for r in range(4):
             nc.sync.dma_start(
                 y_sc_raw[32 * r + WB_ROW : 32 * r + WB_ROW + 4, 0 : E * N].bitcast(I32).rearrange("q (e n) -> q e n", e=E),
@@ -103,13 +101,16 @@ def tile_moe_elr_s_relu_kernel(
                 w_scales.rearrange("e s b n -> b (e s) n")[4 * r : 4 * r + 4].bitcast(I32),
             )
 
+        for q in range(4):
+            rows = slice(32 * q, 32 * q + 4 * PASSES)
+            nc.vector.tensor_copy(xs_window[rows, 0:T].bitcast(I32), xs_rows[rows, :].bitcast(I32))
         nc.vector.tensor_copy(xs[:], xs_window[:].indirect(offsets[:]))
-        nc.sync.dma_start(xs_shift[0:SHIFT_ROWS, :].bitcast(I32), xs[4 : 4 + SHIFT_ROWS, :].bitcast(I32))
 
-        late = keep.tile([P, 2 * (E - 1) * N], I32, name="late", tag="reused", align_bytes=64)
-        y_words = late[:]
-        w_raw.extend(y_words[:, 2 * i * N : (2 * i + 1) * N] for i in range(E - 1))
-        wb_raw.extend(y_words[:, (2 * i + 1) * N : (2 * i + 2) * N] for i in range(E - 1))
+        late = keep.tile([P, 2 * E * N], I32, name="late", tag="reused", align_bytes=64)
+        w_raw = [late[:, 2 * e * N : (2 * e + 1) * N] for e in range(E)]
+        wb_raw = [late[:, (2 * e + 1) * N : (2 * e + 2) * N] for e in range(E)]
+        load_y_words(0)
+        nc.sync.dma_start(xs_shift[0:SHIFT_ROWS, :].bitcast(I32), xs[4 : 4 + SHIFT_ROWS, :].bitcast(I32))
         for e in range(1, E):
             load_y_words(e)
         for e in range(E):
@@ -214,11 +215,11 @@ def tile_moe_elr_s_relu_kernel(
             h_product(u)
         h_grouped[1] = h_turn(1)
         h_grouped[2] = h_turn(2)
-        deal(0)
         nc.vector.tensor_copy(
             y_sc[:].rearrange("p g (t m) -> p g t m", t=PACK),
             y_sc_raw[:].rearrange("p (g m t) -> p g t m", g=E * PASSES, t=PACK),
         )
+        deal(0)
         hq_all = keep.tile([P, S], U32, name="hq_all", tag="raw_scales", align_bytes=64)
         hq = [hq_all[:, e * C : (e + 1) * C] for e in range(E)]
         h_quantize(0, h_grouped[0])

@@ -22,7 +22,6 @@ PACK = 4
 PASSES = K // (P * PACK)
 TILES = S // P
 PER = C // P
-WINDOW = 1024
 WA_ROW = 12
 WB_ROW = 4
 SHIFT_ROWS = 100
@@ -40,23 +39,27 @@ def tile_moe_elr_s_relu_kernel(
             return keep.tile(shape, dtype, name=name, align_bytes=64)
 
         offsets = keep.tile([P, S // 16], U16, name="offsets")
-        xs_window = keep.tile([P, WINDOW], U8, name="xs_window", tag="reused", align_bytes=64)
-        xs_rows = held([P, T], U8, "xs_rows")
+        xs_rows = keep.tile([P, T], U8, name="xs_rows", tag="reused", align_bytes=64)
+        xs_window = held([P, T], U8, "xs_window")
         wa_sc = held([P, E * PASSES, H], U8, "wa_sc")
-        y_sc_raw = keep.tile([P, E * PASSES * N], U8, name="y_sc_raw", tag="raw_scales", align_bytes=64)
+        y_sc_raw = held([P, E * PASSES, N], U8, "y_sc_raw")
         xs_shift = held([P, S], U8, "xs_shift")
         xs = held([P, S], U8, "xs")
         ident = held([P, P], F32, "ident")
+        warm_in = held([P, 1], F32, "warm_in")
+        warm_out = held([P, 1], F32, "warm_out")
         x_raw = [held([P, T], I32, f"x_raw{s}") for s in range(PASSES)]
-        early = [held([P, PASSES * H], I32, f"early{i}") for i in range(E)]
+        wa_first = held([P, PASSES * H], I32, "wa_first")
         xg = [[held([P, C], U32, f"xg{e}_{s}") for s in range(PASSES)] for e in range(E)]
         w = [held([P, PASSES, 2 * N], U8, f"w{e}") for e in range(E)]
         wb = [held([P, N], I32, f"wb{e}") for e in range(E)]
-        y_sc = held([P, E * PASSES, N], U8, "y_sc")
+        y_sc = [held([P, PASSES, N], U8, f"y_sc{e}") for e in range(E)]
+        hq = [held([P, C], U32, f"hq{e}")[:] for e in range(E)]
         hq_sc = [held([P, C], U8, f"hq_sc{e}") for e in range(E)]
         yq = held([P, S], U32, "yq")
         yq_sc = held([P, S], U8, "yq_sc")
 
+        nc.gpsimd.memset(warm_in[:], 0.0)
         nc.gpsimd.memset(xs_window[:].bitcast(I32), 0)
         nc.vector.memset(wa_sc[:].bitcast(I32), 0)
         nc.vector.memset(y_sc_raw[:].bitcast(I32), 0)
@@ -74,7 +77,7 @@ def tile_moe_elr_s_relu_kernel(
             )
             nc.sync.dma_start(wb_raw[e], wb_words[e, 0].rearrange("p n d -> p (n d)").bitcast(I32))
 
-        wa = [early[e][:] for e in range(E)]
+        wa = [wa_first[:]]
         nc.sync.dma_start(offsets[:], offs)
         for q in range(4):
             nc.sync.dma_start(
@@ -88,42 +91,53 @@ def tile_moe_elr_s_relu_kernel(
                 wa_sc[32 * q + WA_ROW : 32 * q + WA_ROW + 4, :, :].bitcast(I32),
                 wa_scales.rearrange("e s b i -> b (e s) i")[4 * q : 4 * q + 4].bitcast(I32),
             )
-        load_wa(1)
-        load_wa(2)
+        nc.scalar.activation(warm_out[:], warm_in[:], RELU)
         for r in range(4):
-            nc.sync.dma_start(
-                y_sc_raw[32 * r + WB_ROW : 32 * r + WB_ROW + 4, 0 : E * N].bitcast(I32).rearrange("q (e n) -> q e n", e=E),
+            nc.scalar.dma_start(
+                y_sc_raw[32 * r + WB_ROW : 32 * r + WB_ROW + 4].bitcast(I32).rearrange("q (e s) n -> q e s n", e=E)[:, :, 0, :],
                 wb_scales[:, 0].rearrange("e b n -> b e n")[4 * r : 4 * r + 4].bitcast(I32),
             )
         for r in range(4):
-            nc.sync.dma_start(
-                y_sc_raw[32 * r : 32 * r + 4, :].bitcast(I32).rearrange("q (g n) -> q g n", g=E * PASSES),
+            nc.scalar.dma_start(
+                y_sc_raw[32 * r : 32 * r + 4].bitcast(I32),
                 w_scales.rearrange("e s b n -> b (e s) n")[4 * r : 4 * r + 4].bitcast(I32),
             )
 
         for q in range(4):
             rows = slice(32 * q, 32 * q + 4 * PASSES)
-            nc.vector.tensor_copy(xs_window[rows, 0:T].bitcast(I32), xs_rows[rows, :].bitcast(I32))
-        nc.vector.tensor_copy(xs[:], xs_window[:].indirect(offsets[:]))
+            nc.vector.tensor_copy(xs_window[rows, :].bitcast(I32), xs_rows[rows, :].bitcast(I32))
 
-        late = keep.tile([P, 2 * E * N], I32, name="late", tag="reused", align_bytes=64)
+        late = keep.tile([P, 2 * E * N + (E - 1) * PASSES * H], I32, name="late", tag="reused", align_bytes=64)
         w_raw = [late[:, 2 * e * N : (2 * e + 1) * N] for e in range(E)]
         wb_raw = [late[:, (2 * e + 1) * N : (2 * e + 2) * N] for e in range(E)]
-        load_y_words(0)
-        nc.sync.dma_start(xs_shift[0:SHIFT_ROWS, :].bitcast(I32), xs[4 : 4 + SHIFT_ROWS, :].bitcast(I32))
         for e in range(1, E):
-            load_y_words(e)
+            first = 2 * E * N + (e - 1) * PASSES * H
+            wa.append(late[:, first : first + PASSES * H])
+            load_wa(e)
         for e in range(E):
+            load_y_words(e)
+
+        def gather_scales(lo, hi):
+            nc.vector.tensor_copy(xs[:, lo:hi], xs_window[:].indirect(offsets[:, lo // 16 : hi // 16]))
+
+        def gather_words(e):
             for s in range(PASSES):
                 nc.vector.tensor_copy(
                     xg[e][s][:], x_raw[s][:].bitcast(U32).indirect(offsets[:, e * C // 16 : (e + 1) * C // 16])
                 )
 
+        gather_scales(0, C)
+        gather_words(0)
+        gather_scales(C, S)
+        nc.gpsimd.dma_start(xs_shift[0:SHIFT_ROWS, :].bitcast(I32), xs[4 : 4 + SHIFT_ROWS, :].bitcast(I32))
+        for e in range(1, E):
+            gather_words(e)
+
         h_pairs = {}
 
         def h_product(u):
             e, a = divmod(u, PER)
-            bank = psum.tile([P, H], F32, name="h_bank", tag="sums", bufs=4)
+            bank = psum.tile([P, H], F32, name="h_bank", bufs=3)
             for s in range(PASSES):
                 nc.tensor.matmul_mx(
                     out=bank[:],
@@ -159,6 +173,10 @@ def tile_moe_elr_s_relu_kernel(
 
         def deal(e):
             nc.vector.tensor_copy(
+                y_sc[e][:].rearrange("p s (t m) -> p s t m", t=PACK),
+                y_sc_raw[:, e * PASSES : (e + 1) * PASSES, :].rearrange("p s (m t) -> p s t m", t=PACK),
+            )
+            nc.vector.tensor_copy(
                 w[e][:].bitcast(U16).rearrange("p s (t m) -> p s t m", t=PACK),
                 w_raw[e].bitcast(U16).rearrange("p (s m t) -> p s t m", s=PASSES, t=PACK),
             )
@@ -171,14 +189,14 @@ def tile_moe_elr_s_relu_kernel(
             e, a = divmod(u, PER)
             own = slice(a * P, (a + 1) * P)
             cols = slice(u * P, (u + 1) * P)
-            bank = psum.tile([P, PACK, P], F32, name="y_bank", tag="sums", bufs=4)
+            bank = psum.tile([P, PACK, P], F32, name="y_bank", bufs=3)
             for t in range(PACK):
                 n_cols = slice(t * P, (t + 1) * P)
                 for s in range(PASSES):
                     nc.tensor.matmul_mx(
                         out=bank[:, t, :],
                         lhsT=w[e][:, s, 2 * t * P : 2 * (t + 1) * P].bitcast(FP4X4),
-                        lhsT_scale=y_sc[:, e * PASSES + s, n_cols],
+                        lhsT_scale=y_sc[e][:, s, n_cols],
                         rhs=xg[e][s][:, own].bitcast(FP8X4),
                         rhs_scale=(xs, xs_shift)[s][:, cols],
                         start=(s == 0),
@@ -187,7 +205,7 @@ def tile_moe_elr_s_relu_kernel(
                 nc.tensor.matmul_mx(
                     out=bank[:, t, :],
                     lhsT=wb[e][:, n_cols].bitcast(FP8X4),
-                    lhsT_scale=y_sc[WB_ROW:P, e, n_cols],
+                    lhsT_scale=y_sc[e][WB_ROW:P, 0, n_cols],
                     rhs=hq[e][:, own].bitcast(FP8X4),
                     rhs_scale=hq_sc[e][:, own],
                     start=False,
@@ -215,19 +233,11 @@ def tile_moe_elr_s_relu_kernel(
             h_product(u)
         h_grouped[1] = h_turn(1)
         h_grouped[2] = h_turn(2)
-        nc.vector.tensor_copy(
-            y_sc[:].rearrange("p g (t m) -> p g t m", t=PACK),
-            y_sc_raw[:].rearrange("p (g m t) -> p g t m", g=E * PASSES, t=PACK),
-        )
-        deal(0)
-        hq_all = keep.tile([P, S], U32, name="hq_all", tag="raw_scales", align_bytes=64)
-        hq = [hq_all[:, e * C : (e + 1) * C] for e in range(E)]
-        h_quantize(0, h_grouped[0])
+        for e in range(E):
+            deal(e)
+            h_quantize(e, h_grouped[e])
         for e in range(E):
             ys = [y_product(e * PER + a) for a in range(PER)]
-            if e + 1 < E:
-                deal(e + 1)
-                h_quantize(e + 1, h_grouped[e + 1])
             for a in range(PER):
                 y_quantize(e * PER + a, ys[a])
         for r in range(4):

@@ -22,6 +22,8 @@ PACK = 4
 PASSES = K // (P * PACK)
 TILES = S // P
 PER = C // P
+WINDOW = 1024
+STRETCH = 5120
 WA_ROW = 12
 WB_ROW = 4
 SHIFT_ROWS = 100
@@ -33,37 +35,41 @@ def tile_moe_elr_s_relu_kernel(
     nc = tc.nc
     with ExitStack() as ctx:
         keep = ctx.enter_context(tc.tile_pool(name="keep", bufs=1))
+        chain = ctx.enter_context(tc.tile_pool(name="chain", bufs=1))
         psum = ctx.enter_context(tc.psum_pool(name="psum", bufs=1))
 
         def held(shape, dtype, name):
             return keep.tile(shape, dtype, name=name, align_bytes=64)
 
         offsets = keep.tile([P, S // 16], U16, name="offsets")
-        xs_rows = keep.tile([P, T], U8, name="xs_rows", tag="reused", align_bytes=64)
-        xs_window = held([P, T], U8, "xs_window")
+        xs_rows = held([P, T], U8, "xs_rows")
+        xs_window = keep.tile([P, WINDOW], U8, name="xs_window", tag="reused_window", align_bytes=64)
         wa_sc = held([P, E * PASSES, H], U8, "wa_sc")
         y_sc_raw = held([P, E * PASSES, N], U8, "y_sc_raw")
         xs_shift = held([P, S], U8, "xs_shift")
         xs = held([P, S], U8, "xs")
         ident = held([P, P], F32, "ident")
-        warm_in = held([P, 1], F32, "warm_in")
-        warm_out = held([P, 1], F32, "warm_out")
         x_raw = [held([P, T], I32, f"x_raw{s}") for s in range(PASSES)]
-        wa_first = held([P, PASSES * H], I32, "wa_first")
+        wa = [held([P, PASSES * H], I32, f"wa{e}")[:] for e in range(E)]
+        w_first = held([P, PASSES, N // 2], I32, "w_first")
+        wb_first = held([P, 1, N], I32, "wb_first")
         xg = [[held([P, C], U32, f"xg{e}_{s}") for s in range(PASSES)] for e in range(E)]
-        w = [held([P, PASSES, 2 * N], U8, f"w{e}") for e in range(E)]
-        wb = [held([P, N], I32, f"wb{e}") for e in range(E)]
-        y_sc = [held([P, PASSES, N], U8, f"y_sc{e}") for e in range(E)]
+
+        def placed(shape, dtype, name, e, offset):
+            return chain.tile(shape, dtype, name=name, align_bytes=64, offset=e * STRETCH + offset)
+
+        w = [placed([P, PASSES, 2 * N], U8, f"w{e}", e, 0) for e in range(E)]
+        y_sc = [placed([P, PASSES, N], U8, f"y_sc{e}", e, 2048) for e in range(E)]
+        wb = [placed([P, N], I32, f"wb{e}", e, 3072) for e in range(E)]
         hq = [held([P, C], U32, f"hq{e}")[:] for e in range(E)]
-        hq_sc = [held([P, C], U8, f"hq_sc{e}") for e in range(E)]
+        hq_sc = [y_sc[e][WB_ROW:P, 1, 0:C] for e in range(E)]
         yq = held([P, S], U32, "yq")
         yq_sc = held([P, S], U8, "yq_sc")
 
-        nc.gpsimd.memset(warm_in[:], 0.0)
         nc.gpsimd.memset(xs_window[:].bitcast(I32), 0)
         nc.vector.memset(wa_sc[:].bitcast(I32), 0)
-        nc.vector.memset(y_sc_raw[:].bitcast(I32), 0)
         make_identity(nc, ident[:])
+        nc.vector.memset(y_sc_raw[:].bitcast(I32), 0)
         nc.vector.memset(xs_shift[:].bitcast(I32), 0)
 
         def load_wa(e):
@@ -71,13 +77,16 @@ def tile_moe_elr_s_relu_kernel(
                 wa[e].rearrange("p (s i) -> p s i", s=PASSES), wa_words[e].rearrange("s p i d -> p s (i d)").bitcast(I32)
             )
 
-        def load_y_words(e):
-            nc.sync.dma_start(
-                w_raw[e].rearrange("p (s b) -> p s b", s=PASSES), w_words[e].rearrange("s p b -> p s b").bitcast(I32)
-            )
-            nc.sync.dma_start(wb_raw[e], wb_words[e, 0].rearrange("p n d -> p (n d)").bitcast(I32))
+        def load_y_words(lo, hi, w_tile, wb_tile):
+            nc.sync.dma_start(w_tile, w_words[lo:hi].rearrange("e s p b -> p (e s) b").bitcast(I32))
+            nc.sync.dma_start(wb_tile, wb_words[lo:hi, 0].rearrange("e p n d -> p e (n d)").bitcast(I32))
 
-        wa = [wa_first[:]]
+        def load_wb_scales(q):
+            nc.sync.dma_start(
+                y_sc_raw[32 * q + WB_ROW : 32 * q + WB_ROW + 4].bitcast(I32).rearrange("r (e s) n -> r e s n", e=E)[:, :, 0, :],
+                wb_scales[:, 0].rearrange("e b n -> b e n")[4 * q : 4 * q + 4].bitcast(I32),
+            )
+
         nc.sync.dma_start(offsets[:], offs)
         for q in range(4):
             nc.sync.dma_start(
@@ -87,57 +96,55 @@ def tile_moe_elr_s_relu_kernel(
             nc.sync.dma_start(x_raw[s][:], x_words[s].rearrange("p t d -> p (t d)").bitcast(I32))
         load_wa(0)
         for q in range(4):
-            nc.scalar.dma_start(
+            nc.sync.dma_start(
                 wa_sc[32 * q + WA_ROW : 32 * q + WA_ROW + 4, :, :].bitcast(I32),
                 wa_scales.rearrange("e s b i -> b (e s) i")[4 * q : 4 * q + 4].bitcast(I32),
             )
-        nc.scalar.activation(warm_out[:], warm_in[:], RELU)
-        for r in range(4):
-            nc.scalar.dma_start(
-                y_sc_raw[32 * r + WB_ROW : 32 * r + WB_ROW + 4].bitcast(I32).rearrange("q (e s) n -> q e s n", e=E)[:, :, 0, :],
-                wb_scales[:, 0].rearrange("e b n -> b e n")[4 * r : 4 * r + 4].bitcast(I32),
+        load_wa(1)
+        load_wb_scales(0)
+        load_wb_scales(1)
+        load_wa(2)
+        load_wb_scales(2)
+        load_wb_scales(3)
+        for q in range(4):
+            nc.sync.dma_start(
+                y_sc_raw[32 * q : 32 * q + 4].bitcast(I32),
+                w_scales.rearrange("e s b n -> b (e s) n")[4 * q : 4 * q + 4].bitcast(I32),
             )
-        for r in range(4):
-            nc.scalar.dma_start(
-                y_sc_raw[32 * r : 32 * r + 4].bitcast(I32),
-                w_scales.rearrange("e s b n -> b (e s) n")[4 * r : 4 * r + 4].bitcast(I32),
-            )
+        load_y_words(0, 1, w_first[:], wb_first[:])
 
         for q in range(4):
             rows = slice(32 * q, 32 * q + 4 * PASSES)
-            nc.vector.tensor_copy(xs_window[rows, :].bitcast(I32), xs_rows[rows, :].bitcast(I32))
+            nc.vector.tensor_copy(xs_window[rows, 0:T].bitcast(I32), xs_rows[rows, :].bitcast(I32))
+        nc.vector.tensor_copy(xs[:], xs_window[:].indirect(offsets[:]))
+        nc.sync.dma_start(xs_shift[0:SHIFT_ROWS, :].bitcast(I32), xs[4 : 4 + SHIFT_ROWS, :].bitcast(I32))
+        late = keep.tile([P, 2 * (E - 1) * N], I32, name="late", tag="reused_window", align_bytes=64)
+        load_y_words(
+            1,
+            E,
+            late[:, 0 : (E - 1) * N].rearrange("p (g b) -> p g b", g=(E - 1) * PASSES),
+            late[:, (E - 1) * N :].rearrange("p (e n) -> p e n", e=E - 1),
+        )
+        w_raw = [w_first[:].rearrange("p s b -> p (s b)")] + [late[:, e * N : (e + 1) * N] for e in range(E - 1)]
+        wb_raw = [wb_first[:, 0, :]] + [late[:, (E - 1 + e) * N : (E + e) * N] for e in range(E - 1)]
 
-        late = keep.tile([P, 2 * E * N + (E - 1) * PASSES * H], I32, name="late", tag="reused", align_bytes=64)
-        w_raw = [late[:, 2 * e * N : (2 * e + 1) * N] for e in range(E)]
-        wb_raw = [late[:, (2 * e + 1) * N : (2 * e + 2) * N] for e in range(E)]
-        for e in range(1, E):
-            first = 2 * E * N + (e - 1) * PASSES * H
-            wa.append(late[:, first : first + PASSES * H])
-            load_wa(e)
-        for e in range(E):
-            load_y_words(e)
-
-        def gather_scales(lo, hi):
-            nc.vector.tensor_copy(xs[:, lo:hi], xs_window[:].indirect(offsets[:, lo // 16 : hi // 16]))
-
-        def gather_words(e):
+        def gather_words(e, lo, hi):
             for s in range(PASSES):
                 nc.vector.tensor_copy(
-                    xg[e][s][:], x_raw[s][:].bitcast(U32).indirect(offsets[:, e * C // 16 : (e + 1) * C // 16])
+                    xg[e][s][:, lo:hi],
+                    x_raw[s][:].bitcast(U32).indirect(offsets[:, (e * C + lo) // 16 : (e * C + hi) // 16]),
                 )
 
-        gather_scales(0, C)
-        gather_words(0)
-        gather_scales(C, S)
-        nc.gpsimd.dma_start(xs_shift[0:SHIFT_ROWS, :].bitcast(I32), xs[4 : 4 + SHIFT_ROWS, :].bitcast(I32))
+        gather_words(0, 0, P)
+        gather_words(0, P, C)
         for e in range(1, E):
-            gather_words(e)
+            gather_words(e, 0, C)
 
         h_pairs = {}
 
         def h_product(u):
             e, a = divmod(u, PER)
-            bank = psum.tile([P, H], F32, name="h_bank", bufs=3)
+            bank = psum.tile([P, H], F32, name="h_bank", tag=f"bank{u}")
             for s in range(PASSES):
                 nc.tensor.matmul_mx(
                     out=bank[:],
@@ -156,12 +163,12 @@ def tile_moe_elr_s_relu_kernel(
             )
 
         def h_turn(e):
-            bank = psum.tile([P, PER, 2, P], F32, name="ht_bank", bufs=2)
+            bank = psum.tile([P, PER, 2, P], F32, name="ht_bank", tag=f"bank{4 + e}")
             for a in range(PER):
                 words = h_pairs[e * PER + a][:].bitcast(F32)
                 for v in range(2):
                     nc.tensor.transpose(bank[:, a, v, :], words[:, v * P : (v + 1) * P], ident[:])
-            grouped = held([P, C * PACK], BF16, f"h_grouped{e}")
+            grouped = placed([P, C * PACK], BF16, f"h_grouped{e}", e + 1, 1536)
             nc.scalar.copy(
                 grouped[:].bitcast(F32).rearrange("p (a j v) -> p a j v", a=PER, v=2),
                 bank[:].rearrange("p a v j -> p a j v"),
@@ -169,32 +176,31 @@ def tile_moe_elr_s_relu_kernel(
             return grouped
 
         def h_quantize(e, grouped):
-            nc.vector.quantize_mx(out=hq[e].bitcast(FP8X4), scales=hq_sc[e][:], in_=grouped[:])
+            nc.vector.quantize_mx(out=hq[e].bitcast(FP8X4), scales=hq_sc[e], in_=grouped[:])
 
         def deal(e):
             nc.vector.tensor_copy(
-                y_sc[e][:].rearrange("p s (t m) -> p s t m", t=PACK),
-                y_sc_raw[:, e * PASSES : (e + 1) * PASSES, :].rearrange("p s (m t) -> p s t m", t=PACK),
+                y_sc[e][:].rearrange("p s (t c i) -> p s c t i", t=PACK, i=16),
+                y_sc_raw[:, e * PASSES : (e + 1) * PASSES, :].rearrange("p s (c i t) -> p s c t i", t=PACK, i=16),
             )
             nc.vector.tensor_copy(
-                w[e][:].bitcast(U16).rearrange("p s (t m) -> p s t m", t=PACK),
-                w_raw[e].bitcast(U16).rearrange("p (s m t) -> p s t m", s=PASSES, t=PACK),
+                w[e][:].bitcast(U16).rearrange("p s (t c i) -> p s c t i", t=PACK, i=8),
+                w_raw[e].bitcast(U16).rearrange("p (s c i t) -> p s c t i", s=PASSES, t=PACK, i=8),
             )
             nc.vector.tensor_copy(
                 wb[e][:].rearrange("p (t c i) -> p c t i", t=PACK, i=4),
                 wb_raw[e].rearrange("p (c i t) -> p c t i", t=PACK, i=4),
             )
 
-        def y_product(u):
+        def y_sums(u, bank, ts):
             e, a = divmod(u, PER)
             own = slice(a * P, (a + 1) * P)
             cols = slice(u * P, (u + 1) * P)
-            bank = psum.tile([P, PACK, P], F32, name="y_bank", bufs=3)
-            for t in range(PACK):
+            for place, t in enumerate(ts):
                 n_cols = slice(t * P, (t + 1) * P)
                 for s in range(PASSES):
                     nc.tensor.matmul_mx(
-                        out=bank[:, t, :],
+                        out=bank[:, place, :],
                         lhsT=w[e][:, s, 2 * t * P : 2 * (t + 1) * P].bitcast(FP4X4),
                         lhsT_scale=y_sc[e][:, s, n_cols],
                         rhs=xg[e][s][:, own].bitcast(FP8X4),
@@ -203,7 +209,7 @@ def tile_moe_elr_s_relu_kernel(
                         stop=False,
                     )
                 nc.tensor.matmul_mx(
-                    out=bank[:, t, :],
+                    out=bank[:, place, :],
                     lhsT=wb[e][:, n_cols].bitcast(FP8X4),
                     lhsT_scale=y_sc[e][WB_ROW:P, 0, n_cols],
                     rhs=hq[e][:, own].bitcast(FP8X4),
@@ -211,34 +217,52 @@ def tile_moe_elr_s_relu_kernel(
                     start=False,
                     stop=True,
                 )
-            y = held([P, PACK, P], F32, f"y{u}")
-            grouped = held([P, P * PACK], BF16, f"y_grouped{u}")
-            nc.scalar.copy(y[:], bank[:])
-            nc.sync.dma_start(out_0.rearrange("(p t) j -> p t j", t=PACK)[:, :, cols], y[:])
-            nc.vector.tensor_copy(
-                grouped[:].rearrange("p (c i t) -> p c t i", i=4, t=PACK), y[:].rearrange("p t (c i) -> p c t i", i=4)
-            )
-            return grouped
 
-        def y_quantize(u, grouped):
+        out_rows = out_0.rearrange("(p t) j -> p t j", t=PACK)
+
+        y_grouped = [held([P, C * PACK], BF16, f"y_grouped{e}") for e in range(E)]
+
+        def y_product(u):
+            e, a = divmod(u, PER)
             cols = slice(u * P, (u + 1) * P)
-            nc.vector.quantize_mx(out=yq[:, cols].bitcast(FP8X4), scales=yq_sc[:, cols], in_=grouped[:])
+            y = held([P, PACK, P], F32, f"y{u}")
+            grouped = y_grouped[e][:, a * P * PACK : (a + 1) * P * PACK]
+            bank = psum.tile([P, PACK, P], F32, name="y_bank", tag=f"bank{(6 + u) % 8}")
+            y_sums(u, bank, range(PACK))
+            nc.scalar.copy(y[:], bank[:])
+            nc.sync.dma_start(out_rows[:, :, cols], y[:])
+            nc.vector.tensor_copy(
+                grouped.rearrange("p (c i t) -> p c t i", i=4, t=PACK), y[:].rearrange("p t (c i) -> p c t i", i=4)
+            )
+
+        def y_quantize(e, lo, hi):
+            cols = slice(e * C + lo, e * C + hi)
+            nc.vector.quantize_mx(
+                out=yq[:, cols].bitcast(FP8X4), scales=yq_sc[:, cols], in_=y_grouped[e][:, lo * PACK : hi * PACK]
+            )
             nc.sync.dma_start(out_1[0].rearrange("p j d -> p (j d)").bitcast(I32)[:, cols], yq[:, cols].bitcast(I32))
 
         h_grouped = {}
         for u in range(4):
             h_product(u)
         h_grouped[0] = h_turn(0)
+        h_grouped[1] = h_turn(1)
         for u in range(4, 6):
             h_product(u)
-        h_grouped[1] = h_turn(1)
-        h_grouped[2] = h_turn(2)
-        for e in range(E):
+        for e in range(2):
             deal(e)
             h_quantize(e, h_grouped[e])
-        for e in range(E):
-            ys = [y_product(e * PER + a) for a in range(PER)]
-            for a in range(PER):
-                y_quantize(e * PER + a, ys[a])
+        y_product(0)
+        y_product(1)
+        h_grouped[2] = h_turn(2)
+        deal(2)
+        h_quantize(2, h_grouped[2])
+        y_quantize(0, 0, C)
+        y_product(2)
+        y_product(3)
+        y_product(4)
+        y_quantize(1, 0, C)
+        y_product(5)
+        y_quantize(2, 0, C)
         for r in range(4):
             (nc.sync, nc.scalar)[r % 2].dma_start(out_2[0, 4 * r : 4 * r + 4, :].bitcast(I32), yq_sc[32 * r : 32 * r + 4, :].bitcast(I32))

@@ -23,7 +23,7 @@ PASSES = K // (P * PACK)
 TILES = S // P
 PER = C // P
 WINDOW = 1024
-STRETCH = 5120
+WARM_PASSES = 4
 WA_ROW = 12
 WB_ROW = 4
 SHIFT_ROWS = 100
@@ -41,45 +41,49 @@ def tile_moe_elr_s_relu_kernel(
         def held(shape, dtype, name):
             return keep.tile(shape, dtype, name=name, align_bytes=64)
 
+        def at(shape, dtype, name, offset):
+            return chain.tile(shape, dtype, name=name, align_bytes=64, offset=offset)
+
         offsets = keep.tile([P, S // 16], U16, name="offsets")
         xs_rows = held([P, T], U8, "xs_rows")
-        xs_window = keep.tile([P, WINDOW], U8, name="xs_window", tag="reused_window", align_bytes=64)
-        wa_sc = held([P, E * PASSES, H], U8, "wa_sc")
+        xs_window = at([P, WINDOW], U8, "xs_window", 4096)
+        wa_sc = held([P, E * PASSES + 1, H], U8, "wa_sc")
         y_sc_raw = held([P, E * PASSES, N], U8, "y_sc_raw")
         xs_shift = held([P, S], U8, "xs_shift")
         xs = held([P, S], U8, "xs")
         ident = held([P, P], F32, "ident")
-        x_raw = [held([P, T], I32, f"x_raw{s}") for s in range(PASSES)]
-        wa = [held([P, PASSES * H], I32, f"wa{e}")[:] for e in range(E)]
+        x_raw = held([P, PASSES, T], I32, "x_raw")
+        wa_first = held([P, PASSES, H], I32, "wa_first")
+        wa_rest = held([P, (E - 1) * PASSES, H], I32, "wa_rest")
+        wa = [wa_first[:]] + [wa_rest[:, e * PASSES : (e + 1) * PASSES, :] for e in range(E - 1)]
         w_first = held([P, PASSES, N // 2], I32, "w_first")
         wb_first = held([P, 1, N], I32, "wb_first")
         xg = [[held([P, C], U32, f"xg{e}_{s}") for s in range(PASSES)] for e in range(E)]
 
-        def placed(shape, dtype, name, e, offset):
-            return chain.tile(shape, dtype, name=name, align_bytes=64, offset=e * STRETCH + offset)
-
-        w = [placed([P, PASSES, 2 * N], U8, f"w{e}", e, 0) for e in range(E)]
-        y_sc = [placed([P, PASSES, N], U8, f"y_sc{e}", e, 2048) for e in range(E)]
-        wb = [placed([P, N], I32, f"wb{e}", e, 3072) for e in range(E)]
-        hq = [held([P, C], U32, f"hq{e}")[:] for e in range(E)]
-        hq_sc = [y_sc[e][WB_ROW:P, 1, 0:C] for e in range(E)]
-        yq = held([P, S], U32, "yq")
+        w = [held([P, PASSES, 2 * N], U8, "w0"), at([P, PASSES, 2 * N], U8, "w1", 11776), at([P, PASSES, 2 * N], U8, "w2", 7680)]
+        y_sc = [held([P, PASSES, N], U8, "y_sc0"), at([P, PASSES, N], U8, "y_sc1", 13824), at([P, PASSES, N], U8, "y_sc2", 3072)]
+        wb = [held([P, N], I32, "wb0"), at([P, N], I32, "wb1", 14848), at([P, N], I32, "wb2", 16896)]
+        grouped_at = [13312, 16896, 18944]
+        hq = [held([P, C], U32, "hq0")[:], at([P, C], U32, "hq1", 9728)[:], at([P, C], U32, "hq2", 4608)[:]]
+        hq_sc = [y_sc[0][WB_ROW:P, 1, 0:C]] + [held([P, C], U8, f"hq_sc{e}")[:] for e in range(1, E)]
+        yq = at([P, S], U32, "yq", 0)
         yq_sc = held([P, S], U8, "yq_sc")
 
         nc.gpsimd.memset(xs_window[:].bitcast(I32), 0)
-        nc.vector.memset(wa_sc[:].bitcast(I32), 0)
+        nc.vector.memset(wa_sc[:, 0 : E * PASSES, :].bitcast(I32), 0)
         make_identity(nc, ident[:])
         nc.vector.memset(y_sc_raw[:].bitcast(I32), 0)
         nc.vector.memset(xs_shift[:].bitcast(I32), 0)
+        nc.vector.memset(wa_sc[:, E * PASSES, :].bitcast(I32), 0)
 
-        def load_wa(e):
-            nc.sync.dma_start(
-                wa[e].rearrange("p (s i) -> p s i", s=PASSES), wa_words[e].rearrange("s p i d -> p s (i d)").bitcast(I32)
-            )
+        def load_wa(lo, hi, tile):
+            nc.sync.dma_start(tile[:], wa_words[lo:hi].rearrange("e s p i d -> p (e s) (i d)").bitcast(I32))
 
-        def load_y_words(lo, hi, w_tile, wb_tile):
-            nc.sync.dma_start(w_tile, w_words[lo:hi].rearrange("e s p b -> p (e s) b").bitcast(I32))
-            nc.sync.dma_start(wb_tile, wb_words[lo:hi, 0].rearrange("e p n d -> p e (n d)").bitcast(I32))
+        def load_w(lo, hi, place):
+            nc.sync.dma_start(place, w_words[lo:hi].rearrange("e s p b -> p (e s) b").bitcast(I32))
+
+        def load_wb(lo, hi, place):
+            nc.sync.dma_start(place, wb_words[lo:hi, 0].rearrange("e p n d -> p e (n d)").bitcast(I32))
 
         def load_wb_scales(q):
             nc.sync.dma_start(
@@ -92,47 +96,43 @@ def tile_moe_elr_s_relu_kernel(
             nc.sync.dma_start(
                 xs_rows[32 * q : 32 * q + 4 * PASSES, :].bitcast(I32), x_scales[:, 4 * q : 4 * q + 4, :].bitcast(I32)
             )
-        for s in range(PASSES):
-            nc.sync.dma_start(x_raw[s][:], x_words[s].rearrange("p t d -> p (t d)").bitcast(I32))
-        load_wa(0)
+        load_wa(0, 1, wa_first)
+        nc.sync.dma_start(x_raw[:], x_words.rearrange("s p t d -> p s (t d)").bitcast(I32))
         for q in range(4):
             nc.sync.dma_start(
-                wa_sc[32 * q + WA_ROW : 32 * q + WA_ROW + 4, :, :].bitcast(I32),
+                wa_sc[32 * q + WA_ROW : 32 * q + WA_ROW + 4, 0 : E * PASSES, :].bitcast(I32),
                 wa_scales.rearrange("e s b i -> b (e s) i")[4 * q : 4 * q + 4].bitcast(I32),
             )
-        load_wa(1)
-        load_wb_scales(0)
-        load_wb_scales(1)
-        load_wa(2)
-        load_wb_scales(2)
+        load_wa(1, E, wa_rest)
+        for q in range(3):
+            load_wb_scales(q)
+        for q in range(4):
+            rows = slice(32 * q, 32 * q + 4 * PASSES)
+            nc.vector.tensor_copy(xs_window[rows, 0:T].bitcast(I32), xs_rows[rows, :].bitcast(I32))
+        nc.vector.tensor_copy(xs[:], xs_window[:].indirect(offsets[:]))
+        nc.sync.dma_start(xs_shift[0:SHIFT_ROWS, :].bitcast(I32), xs[4 : 4 + SHIFT_ROWS, :].bitcast(I32))
+        load_w(0, 1, w_first[:])
+        load_wb(0, 1, wb_first[:])
         load_wb_scales(3)
         for q in range(4):
             nc.sync.dma_start(
                 y_sc_raw[32 * q : 32 * q + 4].bitcast(I32),
                 w_scales.rearrange("e s b n -> b (e s) n")[4 * q : 4 * q + 4].bitcast(I32),
             )
-        load_y_words(0, 1, w_first[:], wb_first[:])
 
-        for q in range(4):
-            rows = slice(32 * q, 32 * q + 4 * PASSES)
-            nc.vector.tensor_copy(xs_window[rows, 0:T].bitcast(I32), xs_rows[rows, :].bitcast(I32))
-        nc.vector.tensor_copy(xs[:], xs_window[:].indirect(offsets[:]))
-        nc.sync.dma_start(xs_shift[0:SHIFT_ROWS, :].bitcast(I32), xs[4 : 4 + SHIFT_ROWS, :].bitcast(I32))
-        late = keep.tile([P, 2 * (E - 1) * N], I32, name="late", tag="reused_window", align_bytes=64)
-        load_y_words(
-            1,
-            E,
-            late[:, 0 : (E - 1) * N].rearrange("p (g b) -> p g b", g=(E - 1) * PASSES),
-            late[:, (E - 1) * N :].rearrange("p (e n) -> p e n", e=E - 1),
-        )
-        w_raw = [w_first[:].rearrange("p s b -> p (s b)")] + [late[:, e * N : (e + 1) * N] for e in range(E - 1)]
-        wb_raw = [wb_first[:, 0, :]] + [late[:, (E - 1 + e) * N : (E + e) * N] for e in range(E - 1)]
+        w_late = [at([P, PASSES, N // 2], I32, "w_raw1", 7680), at([P, PASSES, N // 2], I32, "w_raw2", 2560)]
+        wb_late = [at([P, 1, N], I32, "wb_raw1", 9728), at([P, 1, N], I32, "wb_raw2", 4608)]
+        for e in range(1, E):
+            load_w(e, e + 1, w_late[e - 1][:])
+            load_wb(e, e + 1, wb_late[e - 1][:])
+        w_raw = [tile[:].rearrange("p s b -> p (s b)") for tile in [w_first] + w_late]
+        wb_raw = [tile[:, 0, :] for tile in [wb_first] + wb_late]
 
         def gather_words(e, lo, hi):
             for s in range(PASSES):
                 nc.vector.tensor_copy(
                     xg[e][s][:, lo:hi],
-                    x_raw[s][:].bitcast(U32).indirect(offsets[:, (e * C + lo) // 16 : (e * C + hi) // 16]),
+                    x_raw[:, s, :].bitcast(U32).indirect(offsets[:, (e * C + lo) // 16 : (e * C + hi) // 16]),
                 )
 
         gather_words(0, 0, P)
@@ -150,7 +150,7 @@ def tile_moe_elr_s_relu_kernel(
                     out=bank[:],
                     lhsT=xg[e][s][:, a * P : (a + 1) * P].bitcast(FP8X4),
                     lhsT_scale=xs[4 * s : P, u * P : (u + 1) * P],
-                    rhs=wa[e][:, s * H : (s + 1) * H].bitcast(FP8X4),
+                    rhs=wa[e][:, s, :].bitcast(FP8X4),
                     rhs_scale=wa_sc[WA_ROW:P, e * PASSES + s, :],
                     start=(s == 0),
                     stop=(s == PASSES - 1),
@@ -163,12 +163,12 @@ def tile_moe_elr_s_relu_kernel(
             )
 
         def h_turn(e):
-            bank = psum.tile([P, PER, 2, P], F32, name="ht_bank", tag=f"bank{4 + e}")
+            bank = psum.tile([P, PER, 2, P], F32, name="ht_bank", tag=f"bank{e}")
             for a in range(PER):
                 words = h_pairs[e * PER + a][:].bitcast(F32)
                 for v in range(2):
                     nc.tensor.transpose(bank[:, a, v, :], words[:, v * P : (v + 1) * P], ident[:])
-            grouped = placed([P, C * PACK], BF16, f"h_grouped{e}", e + 1, 1536)
+            grouped = at([P, C * PACK], BF16, f"h_grouped{e}", grouped_at[e])
             nc.scalar.copy(
                 grouped[:].bitcast(F32).rearrange("p (a j v) -> p a j v", a=PER, v=2),
                 bank[:].rearrange("p a v j -> p a j v"),
@@ -178,62 +178,79 @@ def tile_moe_elr_s_relu_kernel(
         def h_quantize(e, grouped):
             nc.vector.quantize_mx(out=hq[e].bitcast(FP8X4), scales=hq_sc[e], in_=grouped[:])
 
-        def deal(e):
+        def deal_scales(e):
             nc.vector.tensor_copy(
                 y_sc[e][:].rearrange("p s (t c i) -> p s c t i", t=PACK, i=16),
                 y_sc_raw[:, e * PASSES : (e + 1) * PASSES, :].rearrange("p s (c i t) -> p s c t i", t=PACK, i=16),
             )
+
+        def deal_w(e):
             nc.vector.tensor_copy(
                 w[e][:].bitcast(U16).rearrange("p s (t c i) -> p s c t i", t=PACK, i=8),
                 w_raw[e].bitcast(U16).rearrange("p (s c i t) -> p s c t i", s=PASSES, t=PACK, i=8),
             )
+
+        def deal_wb(e):
             nc.vector.tensor_copy(
                 wb[e][:].rearrange("p (t c i) -> p c t i", t=PACK, i=4),
                 wb_raw[e].rearrange("p (c i t) -> p c t i", t=PACK, i=4),
             )
 
-        def y_sums(u, bank, ts):
+        y_banks = {}
+
+        def y_frozen(u):
             e, a = divmod(u, PER)
             own = slice(a * P, (a + 1) * P)
             cols = slice(u * P, (u + 1) * P)
-            for place, t in enumerate(ts):
-                n_cols = slice(t * P, (t + 1) * P)
-                for s in range(PASSES):
+            bank = psum.tile([P, PACK, P], F32, name="y_bank", tag=f"bank{(6 + u) % 8}")
+            y_banks[u] = bank
+            for s in range(PASSES):
+                for t in reversed(range(PACK)):
                     nc.tensor.matmul_mx(
-                        out=bank[:, place, :],
+                        out=bank[:, t, :],
                         lhsT=w[e][:, s, 2 * t * P : 2 * (t + 1) * P].bitcast(FP4X4),
-                        lhsT_scale=y_sc[e][:, s, n_cols],
+                        lhsT_scale=y_sc[e][:, s, t * P : (t + 1) * P],
                         rhs=xg[e][s][:, own].bitcast(FP8X4),
                         rhs_scale=(xs, xs_shift)[s][:, cols],
-                        start=(s == 0),
+                        start=(s == 0 and t == PACK - 1),
                         stop=False,
                     )
+
+        def y_adapter(u):
+            e, a = divmod(u, PER)
+            own = slice(a * P, (a + 1) * P)
+            bank = y_banks[u]
+            for t in range(PACK):
                 nc.tensor.matmul_mx(
-                    out=bank[:, place, :],
-                    lhsT=wb[e][:, n_cols].bitcast(FP8X4),
-                    lhsT_scale=y_sc[e][WB_ROW:P, 0, n_cols],
+                    out=bank[:, t, :],
+                    lhsT=wb[e][:, t * P : (t + 1) * P].bitcast(FP8X4),
+                    lhsT_scale=y_sc[e][WB_ROW:P, 0, t * P : (t + 1) * P],
                     rhs=hq[e][:, own].bitcast(FP8X4),
                     rhs_scale=hq_sc[e][:, own],
                     start=False,
-                    stop=True,
+                    stop=(t == PACK - 1),
                 )
 
         out_rows = out_0.rearrange("(p t) j -> p t j", t=PACK)
 
-        y_grouped = [held([P, C * PACK], BF16, f"y_grouped{e}") for e in range(E)]
+        y_grouped = [
+            held([P, C * PACK], BF16, "y_grouped0"),
+            at([P, C * PACK], BF16, "y_grouped1", 5632),
+            held([P, C * PACK], BF16, "y_grouped2"),
+        ]
 
         def y_product(u):
-            e, a = divmod(u, PER)
             cols = slice(u * P, (u + 1) * P)
             y = held([P, PACK, P], F32, f"y{u}")
-            grouped = y_grouped[e][:, a * P * PACK : (a + 1) * P * PACK]
-            bank = psum.tile([P, PACK, P], F32, name="y_bank", tag=f"bank{(6 + u) % 8}")
-            y_sums(u, bank, range(PACK))
-            nc.scalar.copy(y[:], bank[:])
+            y_adapter(u)
+            nc.scalar.copy(y[:], y_banks[u][:])
             nc.sync.dma_start(out_rows[:, :, cols], y[:])
-            nc.vector.tensor_copy(
-                grouped.rearrange("p (c i t) -> p c t i", i=4, t=PACK), y[:].rearrange("p t (c i) -> p c t i", i=4)
-            )
+            return y
+
+        def y_round(u, y, copy):
+            e, a = divmod(u, PER)
+            grouped = y_grouped[e][:, a * P * PACK : (a + 1) * P * PACK]
+            copy(grouped.rearrange("p (c i t) -> p c t i", i=4, t=PACK), y[:].rearrange("p t (c i) -> p c t i", i=4))
 
         def y_quantize(e, lo, hi):
             cols = slice(e * C + lo, e * C + hi)
@@ -242,27 +259,51 @@ def tile_moe_elr_s_relu_kernel(
             )
             nc.sync.dma_start(out_1[0].rearrange("p j d -> p (j d)").bitcast(I32)[:, cols], yq[:, cols].bitcast(I32))
 
+        warm = psum.tile([P, H], F32, name="warm", tag="bank7")
+        for i in range(WARM_PASSES):
+            nc.tensor.matmul_mx(
+                out=warm[:],
+                lhsT=wa_first[:, 0, 0:P].bitcast(FP8X4),
+                lhsT_scale=wa_sc[:, E * PASSES, 0:P],
+                rhs=wa_first[:, 0, :].bitcast(FP8X4),
+                rhs_scale=wa_sc[:, E * PASSES, :],
+                start=True,
+                stop=True,
+            )
         h_grouped = {}
-        for u in range(4):
+        for u in range(2 * PER):
             h_product(u)
         h_grouped[0] = h_turn(0)
-        h_grouped[1] = h_turn(1)
-        for u in range(4, 6):
+        for u in range(2 * PER, TILES):
             h_product(u)
-        for e in range(2):
-            deal(e)
-            h_quantize(e, h_grouped[e])
-        y_product(0)
-        y_product(1)
-        h_grouped[2] = h_turn(2)
-        deal(2)
-        h_quantize(2, h_grouped[2])
+        for e in range(1, E):
+            h_grouped[e] = h_turn(e)
+        def y_frozen_pair(e):
+            for u in range(e * PER, (e + 1) * PER):
+                y_frozen(u)
+
+        def y_finish(e, copy):
+            for u in range(e * PER, (e + 1) * PER):
+                y_round(u, y_product(u), copy)
+
+        deal_w(0)
+        deal_wb(0)
+        deal_scales(0)
+        h_quantize(0, h_grouped[0])
+        y_frozen_pair(0)
+        y_finish(0, nc.scalar.copy)
+        deal_w(1)
+        deal_scales(1)
+        deal_wb(1)
+        deal_w(2)
+        h_quantize(1, h_grouped[1])
+        deal_scales(2)
+        deal_wb(2)
         y_quantize(0, 0, C)
-        y_product(2)
-        y_product(3)
-        y_product(4)
-        y_quantize(1, 0, C)
-        y_product(5)
-        y_quantize(2, 0, C)
+        h_quantize(2, h_grouped[2])
+        for e in range(1, E):
+            y_frozen_pair(e)
+            y_finish(e, nc.vector.tensor_copy)
+            y_quantize(e, 0, C)
         for r in range(4):
             (nc.sync, nc.scalar)[r % 2].dma_start(out_2[0, 4 * r : 4 * r + 4, :].bitcast(I32), yq_sc[32 * r : 32 * r + 4, :].bitcast(I32))

@@ -23,7 +23,6 @@ PASSES = K // (P * PACK)
 TILES = S // P
 PER = C // P
 WINDOW = 1024
-WARM_PASSES = 4
 WA_ROW = 12
 WB_ROW = 4
 SHIFT_ROWS = 100
@@ -47,37 +46,34 @@ def tile_moe_elr_s_relu_kernel(
         offsets = keep.tile([P, S // 16], U16, name="offsets")
         xs_rows = held([P, T], U8, "xs_rows")
         xs_window = at([P, WINDOW], U8, "xs_window", 4096)
-        wa_sc = held([P, E * PASSES + 1, H], U8, "wa_sc")
+        wa_sc = held([P, E * PASSES, H], U8, "wa_sc")
         y_sc_raw = held([P, E * PASSES, N], U8, "y_sc_raw")
         xs_shift = held([P, S], U8, "xs_shift")
         xs = held([P, S], U8, "xs")
         ident = held([P, P], F32, "ident")
         x_raw = held([P, PASSES, T], I32, "x_raw")
-        wa_first = held([P, PASSES, H], I32, "wa_first")
-        wa_rest = held([P, (E - 1) * PASSES, H], I32, "wa_rest")
-        wa = [wa_first[:]] + [wa_rest[:, e * PASSES : (e + 1) * PASSES, :] for e in range(E - 1)]
+        wa = [held([P, PASSES, H], I32, f"wa{e}")[:] for e in range(E)]
         w_first = held([P, PASSES, N // 2], I32, "w_first")
         wb_first = held([P, 1, N], I32, "wb_first")
         xg = [[held([P, C], U32, f"xg{e}_{s}") for s in range(PASSES)] for e in range(E)]
 
-        w = [held([P, PASSES, 2 * N], U8, "w0"), at([P, PASSES, 2 * N], U8, "w1", 11776), at([P, PASSES, 2 * N], U8, "w2", 7680)]
-        y_sc = [held([P, PASSES, N], U8, "y_sc0"), at([P, PASSES, N], U8, "y_sc1", 13824), at([P, PASSES, N], U8, "y_sc2", 3072)]
-        wb = [held([P, N], I32, "wb0"), at([P, N], I32, "wb1", 14848), at([P, N], I32, "wb2", 16896)]
-        grouped_at = [13312, 16896, 18944]
-        hq = [held([P, C], U32, "hq0")[:], at([P, C], U32, "hq1", 9728)[:], at([P, C], U32, "hq2", 4608)[:]]
+        w = [held([P, PASSES, 2 * N], U8, "w0"), at([P, PASSES, 2 * N], U8, "w1", 13824), at([P, PASSES, 2 * N], U8, "w2", 9728)]
+        y_sc = [held([P, PASSES, N], U8, "y_sc0"), held([P, PASSES, N], U8, "y_sc1"), held([P, PASSES, N], U8, "y_sc2")]
+        wb = [held([P, N], I32, "wb0"), at([P, N], I32, "wb1", 16896), at([P, N], I32, "wb2", 18944)]
+        grouped_at = [15360, 18944, 20992]
+        hq = [held([P, C], U32, "hq0")[:], at([P, C], U32, "hq1", 11776)[:], at([P, C], U32, "hq2", 4608)[:]]
         hq_sc = [y_sc[0][WB_ROW:P, 1, 0:C]] + [held([P, C], U8, f"hq_sc{e}")[:] for e in range(1, E)]
         yq = at([P, S], U32, "yq", 0)
         yq_sc = held([P, S], U8, "yq_sc")
 
         nc.gpsimd.memset(xs_window[:].bitcast(I32), 0)
-        nc.vector.memset(wa_sc[:, 0 : E * PASSES, :].bitcast(I32), 0)
+        nc.vector.memset(wa_sc[:].bitcast(I32), 0)
         make_identity(nc, ident[:])
         nc.vector.memset(y_sc_raw[:].bitcast(I32), 0)
         nc.vector.memset(xs_shift[:].bitcast(I32), 0)
-        nc.vector.memset(wa_sc[:, E * PASSES, :].bitcast(I32), 0)
 
-        def load_wa(lo, hi, tile):
-            nc.sync.dma_start(tile[:], wa_words[lo:hi].rearrange("e s p i d -> p (e s) (i d)").bitcast(I32))
+        def load_wa(e):
+            nc.sync.dma_start(wa[e], wa_words[e].rearrange("s p i d -> p s (i d)").bitcast(I32))
 
         def load_w(lo, hi, place):
             nc.sync.dma_start(place, w_words[lo:hi].rearrange("e s p b -> p (e s) b").bitcast(I32))
@@ -96,16 +92,22 @@ def tile_moe_elr_s_relu_kernel(
             nc.sync.dma_start(
                 xs_rows[32 * q : 32 * q + 4 * PASSES, :].bitcast(I32), x_scales[:, 4 * q : 4 * q + 4, :].bitcast(I32)
             )
-        load_wa(0, 1, wa_first)
         nc.sync.dma_start(x_raw[:], x_words.rearrange("s p t d -> p s (t d)").bitcast(I32))
+        load_wa(0)
         for q in range(4):
             nc.sync.dma_start(
-                wa_sc[32 * q + WA_ROW : 32 * q + WA_ROW + 4, 0 : E * PASSES, :].bitcast(I32),
+                wa_sc[32 * q + WA_ROW : 32 * q + WA_ROW + 4, :, :].bitcast(I32),
                 wa_scales.rearrange("e s b i -> b (e s) i")[4 * q : 4 * q + 4].bitcast(I32),
             )
-        load_wa(1, E, wa_rest)
-        for q in range(3):
+        for q in range(4):
             load_wb_scales(q)
+        for q in range(4):
+            nc.sync.dma_start(
+                y_sc_raw[32 * q : 32 * q + 4].bitcast(I32),
+                w_scales.rearrange("e s b n -> b (e s) n")[4 * q : 4 * q + 4].bitcast(I32),
+            )
+        load_wa(1)
+        load_wa(2)
         for q in range(4):
             rows = slice(32 * q, 32 * q + 4 * PASSES)
             nc.vector.tensor_copy(xs_window[rows, 0:T].bitcast(I32), xs_rows[rows, :].bitcast(I32))
@@ -113,15 +115,8 @@ def tile_moe_elr_s_relu_kernel(
         nc.sync.dma_start(xs_shift[0:SHIFT_ROWS, :].bitcast(I32), xs[4 : 4 + SHIFT_ROWS, :].bitcast(I32))
         load_w(0, 1, w_first[:])
         load_wb(0, 1, wb_first[:])
-        load_wb_scales(3)
-        for q in range(4):
-            nc.sync.dma_start(
-                y_sc_raw[32 * q : 32 * q + 4].bitcast(I32),
-                w_scales.rearrange("e s b n -> b (e s) n")[4 * q : 4 * q + 4].bitcast(I32),
-            )
-
-        w_late = [at([P, PASSES, N // 2], I32, "w_raw1", 7680), at([P, PASSES, N // 2], I32, "w_raw2", 2560)]
-        wb_late = [at([P, 1, N], I32, "wb_raw1", 9728), at([P, 1, N], I32, "wb_raw2", 4608)]
+        w_late = [at([P, PASSES, N // 2], I32, "w_raw1", 9728), at([P, PASSES, N // 2], I32, "w_raw2", 2560)]
+        wb_late = [at([P, 1, N], I32, "wb_raw1", 11776), at([P, 1, N], I32, "wb_raw2", 4608)]
         for e in range(1, E):
             load_w(e, e + 1, w_late[e - 1][:])
             load_wb(e, e + 1, wb_late[e - 1][:])
@@ -135,9 +130,7 @@ def tile_moe_elr_s_relu_kernel(
                     x_raw[:, s, :].bitcast(U32).indirect(offsets[:, (e * C + lo) // 16 : (e * C + hi) // 16]),
                 )
 
-        gather_words(0, 0, P)
-        gather_words(0, P, C)
-        for e in range(1, E):
+        for e in range(E):
             gather_words(e, 0, C)
 
         h_pairs = {}
@@ -163,7 +156,7 @@ def tile_moe_elr_s_relu_kernel(
             )
 
         def h_turn(e):
-            bank = psum.tile([P, PER, 2, P], F32, name="ht_bank", tag=f"bank{e}")
+            bank = psum.tile([P, PER, 2, P], F32, name="ht_bank", tag=f"bank{3 * e * (e - 1) + e % 2}")
             for a in range(PER):
                 words = h_pairs[e * PER + a][:].bitcast(F32)
                 for v in range(2):
@@ -180,14 +173,14 @@ def tile_moe_elr_s_relu_kernel(
 
         def deal_scales(e):
             nc.vector.tensor_copy(
-                y_sc[e][:].rearrange("p s (t c i) -> p s c t i", t=PACK, i=16),
-                y_sc_raw[:, e * PASSES : (e + 1) * PASSES, :].rearrange("p s (c i t) -> p s c t i", t=PACK, i=16),
+                y_sc[e][:].rearrange("p s (t m) -> p s t m", t=PACK),
+                y_sc_raw[:, e * PASSES : (e + 1) * PASSES, :].rearrange("p s (m t) -> p s t m", t=PACK),
             )
 
         def deal_w(e):
             nc.vector.tensor_copy(
-                w[e][:].bitcast(U16).rearrange("p s (t c i) -> p s c t i", t=PACK, i=8),
-                w_raw[e].bitcast(U16).rearrange("p (s c i t) -> p s c t i", s=PASSES, t=PACK, i=8),
+                w[e][:].bitcast(U16).rearrange("p s (t m) -> p s t m", t=PACK),
+                w_raw[e].bitcast(U16).rearrange("p (s m t) -> p s t m", s=PASSES, t=PACK),
             )
 
         def deal_wb(e):
@@ -240,6 +233,7 @@ def tile_moe_elr_s_relu_kernel(
         ]
 
         def y_product(u):
+            y_frozen(u)
             cols = slice(u * P, (u + 1) * P)
             y = held([P, PACK, P], F32, f"y{u}")
             y_adapter(u)
@@ -257,53 +251,43 @@ def tile_moe_elr_s_relu_kernel(
             nc.vector.quantize_mx(
                 out=yq[:, cols].bitcast(FP8X4), scales=yq_sc[:, cols], in_=y_grouped[e][:, lo * PACK : hi * PACK]
             )
-            nc.sync.dma_start(out_1[0].rearrange("p j d -> p (j d)").bitcast(I32)[:, cols], yq[:, cols].bitcast(I32))
 
-        warm = psum.tile([P, H], F32, name="warm", tag="bank7")
-        for i in range(WARM_PASSES):
-            nc.tensor.matmul_mx(
-                out=warm[:],
-                lhsT=wa_first[:, 0, 0:P].bitcast(FP8X4),
-                lhsT_scale=wa_sc[:, E * PASSES, 0:P],
-                rhs=wa_first[:, 0, :].bitcast(FP8X4),
-                rhs_scale=wa_sc[:, E * PASSES, :],
-                start=True,
-                stop=True,
-            )
+        def store_codes(lo, hi):
+            nc.sync.dma_start(out_1[0].rearrange("p j d -> p (j d)").bitcast(I32)[:, lo:hi], yq[:, lo:hi].bitcast(I32))
+
         h_grouped = {}
         for u in range(2 * PER):
             h_product(u)
         h_grouped[0] = h_turn(0)
         for u in range(2 * PER, TILES):
             h_product(u)
-        for e in range(1, E):
-            h_grouped[e] = h_turn(e)
-        def y_frozen_pair(e):
-            for u in range(e * PER, (e + 1) * PER):
-                y_frozen(u)
-
-        def y_finish(e, copy):
-            for u in range(e * PER, (e + 1) * PER):
-                y_round(u, y_product(u), copy)
-
+        h_grouped[1] = h_turn(1)
+        deal_scales(0)
         deal_w(0)
         deal_wb(0)
-        deal_scales(0)
-        h_quantize(0, h_grouped[0])
-        y_frozen_pair(0)
-        y_finish(0, nc.scalar.copy)
-        deal_w(1)
         deal_scales(1)
+        deal_scales(2)
+        h_quantize(0, h_grouped[0])
+        ys = [y_product(u) for u in range(PER)]
+        h_grouped[2] = h_turn(2)
+        for u in range(PER):
+            y_round(u, ys[u], nc.scalar.copy)
+        deal_w(1)
         deal_wb(1)
         deal_w(2)
         h_quantize(1, h_grouped[1])
-        deal_scales(2)
         deal_wb(2)
-        y_quantize(0, 0, C)
         h_quantize(2, h_grouped[2])
-        for e in range(1, E):
-            y_frozen_pair(e)
-            y_finish(e, nc.vector.tensor_copy)
-            y_quantize(e, 0, C)
+        y_quantize(0, 0, C)
+        store_codes(0, C)
+        for u in range(PER, 2 * PER):
+            y_round(u, y_product(u), nc.vector.tensor_copy)
+        y_quantize(1, 0, C)
+        y_round(TILES - 2, y_product(TILES - 2), nc.vector.tensor_copy)
+        y_quantize(2, 0, P)
+        store_codes(C, S - P)
+        y_round(TILES - 1, y_product(TILES - 1), nc.vector.tensor_copy)
+        y_quantize(2, P, C)
+        store_codes(S - P, S)
         for r in range(4):
             (nc.sync, nc.scalar)[r % 2].dma_start(out_2[0, 4 * r : 4 * r + 4, :].bitcast(I32), yq_sc[32 * r : 32 * r + 4, :].bitcast(I32))

@@ -83,8 +83,8 @@ def tile_moe_elr_s_relu_kernel(
 
         def load_wb_scales(q):
             nc.sync.dma_start(
-                y_sc_raw[32 * q + WB_ROW : 32 * q + WB_ROW + 4].bitcast(I32).rearrange("r (e s) n -> r e s n", e=E)[:, :, 0, :],
-                wb_scales[:, 0].rearrange("e b n -> b e n")[4 * q : 4 * q + 4].bitcast(I32),
+                y_sc_raw[WB_ROW + q : P : 32].bitcast(I32).rearrange("r (e s) n -> r e s n", e=E)[:, :, 0, :],
+                wb_scales[:, 0].rearrange("e b n -> b e n")[q:16:4].bitcast(I32),
             )
 
         nc.sync.dma_start(offsets[:], offs)
@@ -96,15 +96,15 @@ def tile_moe_elr_s_relu_kernel(
         load_wa(0)
         for q in range(4):
             nc.sync.dma_start(
-                wa_sc[32 * q + WA_ROW : 32 * q + WA_ROW + 4, :, :].bitcast(I32),
-                wa_scales.rearrange("e s b i -> b (e s) i")[4 * q : 4 * q + 4].bitcast(I32),
+                wa_sc[WA_ROW + q : P : 32, :, :].bitcast(I32),
+                wa_scales.rearrange("e s b i -> b (e s) i")[q:16:4].bitcast(I32),
             )
         for q in range(4):
             load_wb_scales(q)
         for q in range(4):
             nc.sync.dma_start(
-                y_sc_raw[32 * q : 32 * q + 4].bitcast(I32),
-                w_scales.rearrange("e s b n -> b (e s) n")[4 * q : 4 * q + 4].bitcast(I32),
+                y_sc_raw[q:P:32].bitcast(I32),
+                w_scales.rearrange("e s b n -> b (e s) n")[q:16:4].bitcast(I32),
             )
         load_wa(1)
         load_wa(2)

@@ -92,8 +92,21 @@ def tile_moe_elr_s_relu_kernel(
             nc.sync.dma_start(
                 xs_rows[32 * q : 32 * q + 4 * PASSES, :].bitcast(I32), x_scales[:, 4 * q : 4 * q + 4, :].bitcast(I32)
             )
+        wa0_rows = wa_words[0].rearrange("s p i d -> s p (i d)").bitcast(I32)
+        nc.sync.dma_start(wa[0][:, 0, :], wa0_rows[0])
         nc.sync.dma_start(x_raw[:], x_words.rearrange("s p t d -> p s (t d)").bitcast(I32))
-        load_wa(0)
+        nc.sync.dma_start(wa[0][:, 1, :], wa0_rows[1])
+        warm = psum.tile([P, H], F32, name="warm", tag="bank7")
+        for i in range(6):
+            nc.tensor.matmul_mx(
+                out=warm[:],
+                lhsT=wa[0][:, 0, 0:P].bitcast(FP8X4),
+                lhsT_scale=xs_shift[:, 0:P],
+                rhs=wa[0][:, 0, :].bitcast(FP8X4),
+                rhs_scale=xs_shift[:, 0:H],
+                start=True,
+                stop=True,
+            )
         for q in range(4):
             nc.sync.dma_start(
                 wa_sc[WA_ROW + q : P : 32, :, :].bitcast(I32),

@@ -113,12 +113,12 @@ def tile_moe_elr_s_relu_kernel(
                 wa_scales.rearrange("e s b i -> b (e s) i")[q:16:4].bitcast(I32),
             )
         for q in range(4):
-            load_wb_scales(q)
-        for q in range(4):
             nc.sync.dma_start(
                 y_sc_raw[q:P:32].bitcast(I32),
                 w_scales.rearrange("e s b n -> b (e s) n")[q:16:4].bitcast(I32),
             )
+        for q in range(4):
+            load_wb_scales(q)
         load_wa(1)
         load_wa(2)
         for q in range(4):

@@ -113,7 +113,7 @@ def tile_moe_elr_s_relu_kernel(
                 wa_scales.rearrange("e s b i -> b (e s) i")[q:16:4].bitcast(I32),
             )
         for q in range(4):
-            nc.sync.dma_start(
+            (nc.gpsimd if q < 2 else nc.sync).dma_start(
                 y_sc_raw[q:P:32].bitcast(I32),
                 w_scales.rearrange("e s b n -> b (e s) n")[q:16:4].bitcast(I32),
             )

from contextlib import ExitStack

import concourse.mybir as mybir
from concourse.masks import make_identity

K, T, E, C, H, N = 1024, 768, 3, 256, 512, 512
S = E * C
FLOPS = 2 * S * (K * H + K * N + H * N)

F32 = mybir.dt.float32
BF16 = mybir.dt.bfloat16
I32 = mybir.dt.int32
U32 = mybir.dt.uint32
U16 = mybir.dt.uint16
U8 = mybir.dt.uint8
FP8X4 = mybir.dt.float8_e4m3fn_x4
FP4X4 = mybir.dt.float4_e2m1fn_x4
RELU = mybir.ActivationFunctionType.Relu

P = 128
PACK = 4
PASSES = K // (P * PACK)
TILES = S // P
PER = C // P
WINDOW = 1024
WA_ROW = 12
WB_ROW = 4
SHIFT_ROWS = 100


def tile_moe_elr_s_relu_kernel(
    tc, x_words, x_scales, w_words, w_scales, wa_words, wa_scales, wb_words, wb_scales, offs, out_0, out_1, out_2
):
    nc = tc.nc
    with ExitStack() as ctx:
        keep = ctx.enter_context(tc.tile_pool(name="keep", bufs=1))
        chain = ctx.enter_context(tc.tile_pool(name="chain", bufs=1))
        psum = ctx.enter_context(tc.psum_pool(name="psum", bufs=1))

        def held(shape, dtype, name):
            return keep.tile(shape, dtype, name=name, align_bytes=64)

        def at(shape, dtype, name, offset):
            return chain.tile(shape, dtype, name=name, align_bytes=64, offset=offset)

        offsets = keep.tile([P, S // 16], U16, name="offsets")
        xs_rows = held([P, T], U8, "xs_rows")
        xs_window = at([P, WINDOW], U8, "xs_window", 4096)
        wa_sc = held([P, E * PASSES, H], U8, "wa_sc")
        y_sc_raw = held([P, E * PASSES, N], U8, "y_sc_raw")
        xs_shift = held([P, S], U8, "xs_shift")
        xs = held([P, S], U8, "xs")
        ident = held([P, P], F32, "ident")
        x_raw = held([P, PASSES, T], I32, "x_raw")
        wa = [held([P, PASSES, H], I32, f"wa{e}")[:] for e in range(E)]
        w_first = held([P, PASSES, N // 2], I32, "w_first")
        wb_first = held([P, 1, N], I32, "wb_first")
        xg = [[held([P, C], U32, f"xg{e}_{s}") for s in range(PASSES)] for e in range(E)]

        w = [held([P, PASSES, 2 * N], U8, "w0"), at([P, PASSES, 2 * N], U8, "w1", 13824), at([P, PASSES, 2 * N], U8, "w2", 9728)]
        y_sc = [held([P, PASSES, N], U8, "y_sc0"), held([P, PASSES, N], U8, "y_sc1"), held([P, PASSES, N], U8, "y_sc2")]
        wb = [held([P, N], I32, "wb0"), at([P, N], I32, "wb1", 16896), at([P, N], I32, "wb2", 18944)]
        grouped_at = [15360, 18944, 20992]
        hq = [held([P, C], U32, "hq0")[:], at([P, C], U32, "hq1", 11776)[:], at([P, C], U32, "hq2", 4608)[:]]
        hq_sc = [y_sc[0][WB_ROW:P, 1, 0:C]] + [held([P, C], U8, f"hq_sc{e}")[:] for e in range(1, E)]
        yq = at([P, S], U32, "yq", 0)
        yq_sc = held([P, S], U8, "yq_sc")

        nc.gpsimd.memset(xs_window[:].bitcast(I32), 0)
        nc.vector.memset(wa_sc[:].bitcast(I32), 0)
        make_identity(nc, ident[:])
        nc.vector.memset(y_sc_raw[:].bitcast(I32), 0)
        nc.vector.memset(xs_shift[:].bitcast(I32), 0)

        def load_wa(e):
            nc.sync.dma_start(wa[e], wa_words[e].rearrange("s p i d -> p s (i d)").bitcast(I32))

        def load_w(lo, hi, place):
            nc.sync.dma_start(place, w_words[lo:hi].rearrange("e s p b -> p (e s) b").bitcast(I32))

        def load_wb(lo, hi, place):
            nc.sync.dma_start(place, wb_words[lo:hi, 0].rearrange("e p n d -> p e (n d)").bitcast(I32))

        def load_wb_scales(q):
            nc.sync.dma_start(
                y_sc_raw[WB_ROW + q : P : 32].bitcast(I32).rearrange("r (e s) n -> r e s n", e=E)[:, :, 0, :],
                wb_scales[:, 0].rearrange("e b n -> b e n")[q:16:4].bitcast(I32),
            )

        nc.sync.dma_start(offsets[:], offs)
        for q in range(4):
            nc.sync.dma_start(
                xs_rows[32 * q : 32 * q + 4 * PASSES, :].bitcast(I32), x_scales[:, 4 * q : 4 * q + 4, :].bitcast(I32)
            )
        wa0_rows = wa_words[0].rearrange("s p i d -> s p (i d)").bitcast(I32)
        nc.sync.dma_start(wa[0][:, 0, :], wa0_rows[0])
        nc.sync.dma_start(x_raw[:], x_words.rearrange("s p t d -> p s (t d)").bitcast(I32))
        nc.sync.dma_start(wa[0][:, 1, :], wa0_rows[1])
        warm = psum.tile([P, H], F32, name="warm", tag="bank7")
        for i in range(6):
            nc.tensor.matmul_mx(
                out=warm[:],
                lhsT=wa[0][:, 0, 0:P].bitcast(FP8X4),
                lhsT_scale=xs_shift[:, 0:P],
                rhs=wa[0][:, 0, :].bitcast(FP8X4),
                rhs_scale=xs_shift[:, 0:H],
                start=True,
                stop=True,
            )
        for q in range(4):
            nc.sync.dma_start(
                wa_sc[WA_ROW + q : P : 32, :, :].bitcast(I32),
                wa_scales.rearrange("e s b i -> b (e s) i")[q:16:4].bitcast(I32),
            )
        for q in range(4):
            (nc.gpsimd if q < 2 else nc.sync).dma_start(
                y_sc_raw[q:P:32].bitcast(I32),
                w_scales.rearrange("e s b n -> b (e s) n")[q:16:4].bitcast(I32),
            )
        for q in range(4):
            load_wb_scales(q)
        load_wa(1)
        load_wa(2)
        for q in range(4):
            rows = slice(32 * q, 32 * q + 4 * PASSES)
            nc.vector.tensor_copy(xs_window[rows, 0:T].bitcast(I32), xs_rows[rows, :].bitcast(I32))
        nc.vector.tensor_copy(xs[:], xs_window[:].indirect(offsets[:]))
        nc.sync.dma_start(xs_shift[0:SHIFT_ROWS, :].bitcast(I32), xs[4 : 4 + SHIFT_ROWS, :].bitcast(I32))
        load_w(0, 1, w_first[:])
        load_wb(0, 1, wb_first[:])
        w_late = [at([P, PASSES, N // 2], I32, "w_raw1", 9728), at([P, PASSES, N // 2], I32, "w_raw2", 2560)]
        wb_late = [at([P, 1, N], I32, "wb_raw1", 11776), at([P, 1, N], I32, "wb_raw2", 4608)]
        for e in range(1, E):
            load_w(e, e + 1, w_late[e - 1][:])
            load_wb(e, e + 1, wb_late[e - 1][:])
        w_raw = [tile[:].rearrange("p s b -> p (s b)") for tile in [w_first] + w_late]
        wb_raw = [tile[:, 0, :] for tile in [wb_first] + wb_late]

        def gather_words(e, lo, hi):
            for s in range(PASSES):
                nc.vector.tensor_copy(
                    xg[e][s][:, lo:hi],
                    x_raw[:, s, :].bitcast(U32).indirect(offsets[:, (e * C + lo) // 16 : (e * C + hi) // 16]),
                )

        for e in range(E):
            gather_words(e, 0, C)

        h_pairs = {}

        def h_product(u):
            e, a = divmod(u, PER)
            bank = psum.tile([P, H], F32, name="h_bank", tag=f"bank{u}")
            for s in range(PASSES):
                nc.tensor.matmul_mx(
                    out=bank[:],
                    lhsT=xg[e][s][:, a * P : (a + 1) * P].bitcast(FP8X4),
                    lhsT_scale=xs[4 * s : P, u * P : (u + 1) * P],
                    rhs=wa[e][:, s, :].bitcast(FP8X4),
                    rhs_scale=wa_sc[WA_ROW:P, e * PASSES + s, :],
                    start=(s == 0),
                    stop=(s == PASSES - 1),
                )
            h_pairs[u] = held([P, H], BF16, f"h_pairs{u}")
            nc.scalar.activation(
                h_pairs[u][:].rearrange("j (v p d) -> j v p d", v=2, d=2),
                bank[:].rearrange("j (p v d) -> j v p d", v=2, d=2),
                RELU,
            )

        def h_turn(e):
            bank = psum.tile([P, PER, 2, P], F32, name="ht_bank", tag=f"bank{3 * e * (e - 1) + e % 2}")
            for a in range(PER):
                words = h_pairs[e * PER + a][:].bitcast(F32)
                for v in range(2):
                    nc.tensor.transpose(bank[:, a, v, :], words[:, v * P : (v + 1) * P], ident[:])
            grouped = at([P, C * PACK], BF16, f"h_grouped{e}", grouped_at[e])
            nc.scalar.copy(
                grouped[:].bitcast(F32).rearrange("p (a j v) -> p a j v", a=PER, v=2),
                bank[:].rearrange("p a v j -> p a j v"),
            )
            return grouped

        def h_quantize(e, grouped):
            nc.vector.quantize_mx(out=hq[e].bitcast(FP8X4), scales=hq_sc[e], in_=grouped[:])

        def deal_scales(e):
            nc.vector.tensor_copy(
                y_sc[e][:].rearrange("p s (t m) -> p s t m", t=PACK),
                y_sc_raw[:, e * PASSES : (e + 1) * PASSES, :].rearrange("p s (m t) -> p s t m", t=PACK),
            )

        def deal_w(e):
            nc.vector.tensor_copy(
                w[e][:].bitcast(U16).rearrange("p s (t m) -> p s t m", t=PACK),
                w_raw[e].bitcast(U16).rearrange("p (s m t) -> p s t m", s=PASSES, t=PACK),
            )

        def deal_wb(e):
            nc.vector.tensor_copy(
                wb[e][:].rearrange("p (t c i) -> p c t i", t=PACK, i=4),
                wb_raw[e].rearrange("p (c i t) -> p c t i", t=PACK, i=4),
            )

        y_banks = {}

        def y_frozen(u):
            e, a = divmod(u, PER)
            own = slice(a * P, (a + 1) * P)
            cols = slice(u * P, (u + 1) * P)
            bank = psum.tile([P, PACK, P], F32, name="y_bank", tag=f"bank{(6 + u) % 8}")
            y_banks[u] = bank
            for s in range(PASSES):
                for t in reversed(range(PACK)):
                    nc.tensor.matmul_mx(
                        out=bank[:, t, :],
                        lhsT=w[e][:, s, 2 * t * P : 2 * (t + 1) * P].bitcast(FP4X4),
                        lhsT_scale=y_sc[e][:, s, t * P : (t + 1) * P],
                        rhs=xg[e][s][:, own].bitcast(FP8X4),
                        rhs_scale=(xs, xs_shift)[s][:, cols],
                        start=(s == 0 and t == PACK - 1),
                        stop=False,
                    )

        def y_adapter(u):
            e, a = divmod(u, PER)
            own = slice(a * P, (a + 1) * P)
            bank = y_banks[u]
            for t in range(PACK):
                nc.tensor.matmul_mx(
                    out=bank[:, t, :],
                    lhsT=wb[e][:, t * P : (t + 1) * P].bitcast(FP8X4),
                    lhsT_scale=y_sc[e][WB_ROW:P, 0, t * P : (t + 1) * P],
                    rhs=hq[e][:, own].bitcast(FP8X4),
                    rhs_scale=hq_sc[e][:, own],
                    start=False,
                    stop=(t == PACK - 1),
                )

        out_rows = out_0.rearrange("(p t) j -> p t j", t=PACK)

        y_grouped = [
            held([P, C * PACK], BF16, "y_grouped0"),
            at([P, C * PACK], BF16, "y_grouped1", 5632),
            held([P, C * PACK], BF16, "y_grouped2"),
        ]

        def y_product(u):
            y_frozen(u)
            cols = slice(u * P, (u + 1) * P)
            y = held([P, PACK, P], F32, f"y{u}")
            y_adapter(u)
            nc.scalar.copy(y[:], y_banks[u][:])
            nc.sync.dma_start(out_rows[:, :, cols], y[:])
            return y

        def y_round(u, y, copy):
            e, a = divmod(u, PER)
            grouped = y_grouped[e][:, a * P * PACK : (a + 1) * P * PACK]
            copy(grouped.rearrange("p (c i t) -> p c t i", i=4, t=PACK), y[:].rearrange("p t (c i) -> p c t i", i=4))

        def y_quantize(e, lo, hi):
            cols = slice(e * C + lo, e * C + hi)
            nc.vector.quantize_mx(
                out=yq[:, cols].bitcast(FP8X4), scales=yq_sc[:, cols], in_=y_grouped[e][:, lo * PACK : hi * PACK]
            )

        def store_codes(lo, hi):
            nc.sync.dma_start(out_1[0].rearrange("p j d -> p (j d)").bitcast(I32)[:, lo:hi], yq[:, lo:hi].bitcast(I32))

        h_grouped = {}
        for u in range(2 * PER):
            h_product(u)
        h_grouped[0] = h_turn(0)
        for u in range(2 * PER, TILES):
            h_product(u)
        h_grouped[1] = h_turn(1)
        deal_scales(0)
        deal_w(0)
        deal_wb(0)
        deal_scales(1)
        deal_scales(2)
        h_quantize(0, h_grouped[0])
        ys = [y_product(u) for u in range(PER)]
        h_grouped[2] = h_turn(2)
        for u in range(PER):
            y_round(u, ys[u], nc.scalar.copy)
        deal_w(1)
        deal_wb(1)
        deal_w(2)
        h_quantize(1, h_grouped[1])
        deal_wb(2)
        h_quantize(2, h_grouped[2])
        y_quantize(0, 0, C)
        store_codes(0, C)
        for u in range(PER, 2 * PER):
            y_round(u, y_product(u), nc.vector.tensor_copy)
        y_quantize(1, 0, C)
        y_round(TILES - 2, y_product(TILES - 2), nc.vector.tensor_copy)
        y_quantize(2, 0, P)
        store_codes(C, S - P)
        y_round(TILES - 1, y_product(TILES - 1), nc.vector.tensor_copy)
        y_quantize(2, P, C)
        store_codes(S - P, S)
        for r in range(4):
            (nc.sync, nc.scalar)[r % 2].dma_start(out_2[0, 4 * r : 4 * r + 4, :].bitcast(I32), yq_sc[32 * r : 32 * r + 4, :].bitcast(I32))
